import numpy as np
import ml_dtypes


def mxq(x, axis, fmt="e4m3"):
    dtype, down = {"e4m3": (ml_dtypes.float8_e4m3fn, 7), "e5m2": (ml_dtypes.float8_e5m2, 14)}[fmt]
    v = np.moveaxis(np.asarray(x, np.float32).astype(ml_dtypes.bfloat16).astype(np.float64), axis, -1)
    blocks = v.reshape(v.shape[:-1] + (-1, 32))
    amax = np.abs(blocks).max(-1, keepdims=True)
    byte = np.maximum(np.where(amax > 0, np.frexp(amax)[1] - 1 + 127, 0) - down, 1)
    scale = np.exp2(byte - 127.0)
    codes = (blocks / scale).astype(np.float32).astype(dtype).astype(np.float64)
    return np.moveaxis((codes * scale).reshape(v.shape), -1, axis)


WIDE = False


def mx_kscale(k):
    if not WIDE:
        return np.ones(k)
    levels = np.array([18, -18])
    if k % 512:
        return np.exp2(np.random.permutation(np.resize(levels, k // 32))).repeat(32)
    a = np.empty((k // 512, 16))
    for p in range(k // 512):
        a[p, :8] = np.random.permutation(np.resize(levels, 8))
        for g in range(8):
            far = levels[np.abs(levels - a[p, g]) >= 10]
            a[p, g + 8] = far[np.random.randint(len(far))]
    return np.exp2(a.ravel()).repeat(32)


def f64(x):
    return np.asarray(x).astype(np.float64)


def striped(idx):
    return np.tile(np.asarray(idx).reshape(-1, 16).T, (8, 1)).astype(np.uint16)


def unstriped(offs):
    return offs[:16].T.reshape(-1).astype(np.int64)

def planes(y):
    n, m = y.shape
    v = y.astype(np.float32).astype(ml_dtypes.bfloat16).astype(np.float64).reshape(n // 32, 32, m)
    top = np.abs(v).max(1)
    byte = np.clip(np.where(top > 0, np.frexp(top)[1] - 1 + 127 - 7, 1), 1, 254)
    codes = (v * np.exp2(127.0 - byte)[:, None, :]).reshape(n, m).astype(np.float32).astype(ml_dtypes.float8_e4m3fn).view(np.uint8)
    words = codes.reshape(n // 512, 128, 4, m).transpose(0, 1, 3, 2)
    return np.ascontiguousarray(words), np.ascontiguousarray(byte.astype(np.uint8).reshape(n // 512, 16, m))


def setup_inputs():
    n = np.random.standard_normal
    uni = np.random.uniform
    order = np.random.permutation(2048)
    keep = order[:512]
    gone = order[512:1024]
    f_m = mx_kscale(512)
    return {
        "W": (n((512, 512)) / np.sqrt(512) * f_m[:, None]).astype(np.float32),
        "dz": (n((512, 512)) / f_m[:, None]).astype(np.float32),
        "wk": np.tile(uni(0.3, 0.7, 512), (128, 1)).astype(np.float32),
        "wg": np.tile(uni(0.3, 0.7, 512), (128, 1)).astype(np.float32),
        "koffs": striped(keep),
        "goffs": striped(gone),
    }


def reference(W, dz, wk, wg, koffs, goffs):
    keep = unstriped(koffs)
    gone = unstriped(goffs)
    u = mxq(f64(W), 0, "e4m3").T @ mxq(f64(dz), 0, "e5m2")
    a = f64(wk)[:1] * u
    b = f64(wg)[:1] * u
    pa = np.zeros((512, 2048))
    pa[:, keep] = a
    pb = np.zeros((512, 2048))
    pb[:, gone] = b
    out_0 = pa + pb
    return (out_0,) + planes(out_0)

@@ -1,0 +1,159 @@
+from contextlib import ExitStack
+
+import concourse.mybir as mybir
+
+F32 = mybir.dt.float32
+BF16 = mybir.dt.bfloat16
+I32 = mybir.dt.int32
+U32 = mybir.dt.uint32
+U16 = mybir.dt.uint16
+U8 = mybir.dt.uint8
+E4M3 = mybir.dt.float8_e4m3fn_x4
+E5M2 = mybir.dt.float8_e5m2_x4
+MULT = mybir.AluOpType.mult
+
+P = 128
+LANES = 4
+MERGED = 512
+FEATURES = 512
+TOKENS = 2048
+HALF = 256
+CHUNK = 512
+CHUNKS = TOKENS // CHUNK
+WINDOWS = 3
+LANE_ORDER = (0, 2, 3, 1)
+VECTOR_CHUNKS = 2
+
+FLOPS = 2 * 512 * 512 * 512
+
+
+def tile_attend_gmerge_pl_kernel(tc, W, dz, wk, wg, koffs, goffs, out_0, out_1, out_2):
+    nc = tc.nc
+    with ExitStack() as ctx:
+        pool = ctx.enter_context(tc.tile_pool(name="held", bufs=1))
+        ring = ctx.enter_context(tc.tile_pool(name="ring", bufs=2))
+        psum = ctx.enter_context(tc.psum_pool(name="psum", bufs=1))
+
+        keep_list = pool.tile([P, MERGED // 16], U16, name="keep_list")
+        gone_list = pool.tile([P, MERGED // 16], U16, name="gone_list")
+        keep_weight = pool.tile([P, MERGED], F32, name="keep_weight")
+        gone_weight = pool.tile([P, MERGED], F32, name="gone_weight")
+        dz_rows = dz.rearrange("(p j) i -> p j i", j=LANES)
+        w_rows = W.rearrange("(p j) d -> p j d", j=LANES)
+        dz_raw = [pool.tile([P, LANES, HALF], F32, name=f"dz_raw{h}") for h in range(2)]
+        w_raw = [pool.tile([P, LANES, HALF], F32, name=f"w_raw{h}") for h in range(2)]
+        for h in range(2):
+            nc.sync.dma_start(out=dz_raw[h][:], in_=dz_rows[:, :, h * HALF : (h + 1) * HALF])
+        for h in range(2):
+            nc.sync.dma_start(out=w_raw[h][:], in_=w_rows[:, :, h * HALF : (h + 1) * HALF])
+        nc.sync.dma_start(keep_list[:], koffs)
+        nc.sync.dma_start(out=keep_weight[:], in_=wk)
+        nc.sync.dma_start(gone_list[:], goffs)
+        nc.sync.dma_start(out=gone_weight[:], in_=wg)
+
+        windows = [pool.tile([P, TOKENS], F32, name=f"window{n}") for n in range(WINDOWS)]
+        for window, engine in zip(windows, (nc.vector, nc.gpsimd, nc.vector)):
+            engine.memset(window[:].bitcast(I32), 0)
+
+        dz_codes = pool.tile([P, MERGED], U32, name="dz_codes", align_bytes=64)
+        dz_scales = pool.tile([P, MERGED], U8, name="dz_scales", align_bytes=64)
+        for h, round_and_group in enumerate((nc.scalar.copy, nc.vector.tensor_copy)):
+            grouped = pool.tile([P, HALF * LANES], BF16, name=f"dz_grouped{h}", align_bytes=64)
+            round_and_group(
+                out=grouped[:].rearrange("p (c i j) -> p c j i", i=4, j=LANES),
+                in_=dz_raw[h][:].rearrange("p j (c i) -> p c j i", i=4),
+            )
+            columns = slice(h * HALF, (h + 1) * HALF)
+            nc.vector.quantize_mx(
+                out=dz_codes[:, columns].bitcast(E5M2), scales=dz_scales[:, columns], in_=grouped[:]
+            )
+
+        first = LANE_ORDER[0]
+        w_codes = [pool.tile([P, P], U32, name=f"w_codes{t}", align_bytes=64) for t in range(LANES)]
+        w_scales = [pool.tile([P, P], U8, name=f"w_scales{t}", align_bytes=64) for t in range(LANES)]
+        per_half = HALF // LANES
+        for h, round_and_group in enumerate((nc.scalar.copy, nc.vector.tensor_copy)):
+            grouped = pool.tile([P, per_half * LANES], BF16, name=f"w_first{h}", align_bytes=64)
+            round_and_group(
+                out=grouped[:].rearrange("p (m j) -> p m j", j=LANES),
+                in_=w_raw[h][:].rearrange("p j (m t) -> p t m j", t=LANES)[:, first],
+            )
+            columns = slice(h * per_half, (h + 1) * per_half)
+            nc.vector.quantize_mx(
+                out=w_codes[first][:, columns].bitcast(E4M3), scales=w_scales[first][:, columns], in_=grouped[:]
+            )
+        w_rest = pool.tile([P, (LANES - 1) * P * LANES], BF16, name="w_rest", align_bytes=64)
+        w_rest_view = w_rest[:].rearrange("p (t h m j) -> p h m j t", t=LANES - 1, h=2, j=LANES)
+        for h in range(2):
+            nc.scalar.copy(
+                out=w_rest_view[:, h],
+                in_=w_raw[h][:].rearrange("p j (m t) -> p m j t", t=LANES)[:, :, :, 1:LANES],
+            )
+        for t in LANE_ORDER[1:]:
+            nc.vector.quantize_mx(
+                out=w_codes[t][:].bitcast(E4M3),
+                scales=w_scales[t][:],
+                in_=w_rest[:, (t - 1) * P * LANES : t * P * LANES],
+            )
+
+        acc = {}
+        for t in LANE_ORDER:
+            acc[t] = psum.tile([P, MERGED], F32, name=f"acc{t}")
+            nc.tensor.matmul_mx(
+                out=acc[t][:],
+                lhsT=w_codes[t][:].bitcast(E4M3),
+                lhsT_scale=w_scales[t][:],
+                rhs=dz_codes[:].bitcast(E5M2),
+                rhs_scale=dz_scales[:],
+                start=True,
+                stop=True,
+            )
+
+        def product_in_sbuf(t):
+            u = ring.tile([P, MERGED], F32, name="u")
+            nc.scalar.copy(out=u[:], in_=acc[t][:])
+            return u
+
+        out_rows = out_0.rearrange("(p t) c -> p t c", t=LANES)
+        grouped_out = [
+            pool.tile([P, CHUNK * LANES], BF16, name=f"grouped_out{c}", align_bytes=64) for c in range(CHUNKS)
+        ]
+
+        def round_into_lane(copy, window, t, c):
+            copy(
+                out=grouped_out[c][:].rearrange("p (c t) -> p t c", t=LANES)[:, t],
+                in_=window[:, c * CHUNK : (c + 1) * CHUNK],
+            )
+
+        u_keep = product_in_sbuf(LANE_ORDER[0])
+        u_gone = product_in_sbuf(LANE_ORDER[0])
+        u_next = None
+        for n, t in enumerate(LANE_ORDER):
+            window = windows[n % WINDOWS]
+            nc.vector.tensor_tensor(window[:].indirect(keep_list[:]), u_keep[:], keep_weight[:], MULT)
+            if n == 0:
+                u_next = product_in_sbuf(LANE_ORDER[1])
+            nc.vector.tensor_tensor(window[:].indirect(gone_list[:]), u_gone[:], gone_weight[:], MULT)
+            nc.sync.dma_start(out=out_rows[:, t, :], in_=window[:])
+            u_keep = u_gone = u_next
+            for c in range(CHUNKS):
+                on_vector = n == LANES - 1 and c < VECTOR_CHUNKS
+                round_into_lane(nc.vector.tensor_copy if on_vector else nc.scalar.copy, window, t, c)
+                if c == 0 and n + 2 < LANES:
+                    u_next = product_in_sbuf(LANE_ORDER[n + 2])
+
+        out_words = out_1.rearrange("a p c t -> (a p) (c t)").bitcast(I32)
+        out_scales = pool.tile([P, CHUNK], U8, name="out_scales", align_bytes=64)
+        for c in range(CHUNKS):
+            codes = pool.tile([P, CHUNK], U32, name=f"out_codes{c}", align_bytes=64)
+            nc.vector.quantize_mx(
+                out=codes[:].bitcast(E4M3), scales=out_scales[4 * c : P, :], in_=grouped_out[c][:]
+            )
+            nc.sync.dma_start(out=out_words[:, c * CHUNK : (c + 1) * CHUNK], in_=codes[:].bitcast(I32))
+        scale_rows = out_2.rearrange("a b c -> (a b) c").bitcast(I32).rearrange("b (c w) -> c b w", c=CHUNKS)
+        for q in range(4):
+            queue = nc.sync if q % 2 == 0 else nc.scalar
+            queue.dma_start(
+                out=scale_rows[:, 4 * q : 4 * q + 4, :],
+                in_=out_scales[32 * q : 32 * q + 16, :].bitcast(I32),
+            )

@@ -1,6 +1,7 @@
 from contextlib import ExitStack
 
 import concourse.mybir as mybir
+from concourse.masks import make_identity
 
 F32 = mybir.dt.float32
 BF16 = mybir.dt.bfloat16
@@ -18,11 +19,12 @@ MERGED = 512
 FEATURES = 512
 TOKENS = 2048
 HALF = 256
+GROUPS = FEATURES // P
 CHUNK = 512
 CHUNKS = TOKENS // CHUNK
-WINDOWS = 3
-LANE_ORDER = (0, 2, 3, 1)
+BLOCKS = CHUNK // P
 VECTOR_CHUNKS = 2
+WINDOWS = 2
 
 FLOPS = 2 * 512 * 512 * 512
 
@@ -31,7 +33,6 @@ def tile_attend_gmerge_pl_kernel(tc, W, dz, wk, wg, koffs, goffs, out_0, out_1, 
     nc = tc.nc
     with ExitStack() as ctx:
         pool = ctx.enter_context(tc.tile_pool(name="held", bufs=1))
-        ring = ctx.enter_context(tc.tile_pool(name="ring", bufs=2))
         psum = ctx.enter_context(tc.psum_pool(name="psum", bufs=1))
 
         keep_list = pool.tile([P, MERGED // 16], U16, name="keep_list")
@@ -41,106 +42,155 @@ def tile_attend_gmerge_pl_kernel(tc, W, dz, wk, wg, koffs, goffs, out_0, out_1, 
         dz_rows = dz.rearrange("(p j) i -> p j i", j=LANES)
         w_rows = W.rearrange("(p j) d -> p j d", j=LANES)
         dz_raw = [pool.tile([P, LANES, HALF], F32, name=f"dz_raw{h}") for h in range(2)]
-        w_raw = [pool.tile([P, LANES, HALF], F32, name=f"w_raw{h}") for h in range(2)]
-        for h in range(2):
-            nc.sync.dma_start(out=dz_raw[h][:], in_=dz_rows[:, :, h * HALF : (h + 1) * HALF])
-        for h in range(2):
-            nc.sync.dma_start(out=w_raw[h][:], in_=w_rows[:, :, h * HALF : (h + 1) * HALF])
+        w_raw = [pool.tile([P, LANES, HALF], F32, name=f"w_raw{h}", align_bytes=64) for h in range(2)]
+        nc.sync.dma_start(out=dz_raw[0][:], in_=dz_rows[:, :, 0:HALF])
+        nc.sync.dma_start(out=w_raw[0][:], in_=w_rows[:, :, 0:HALF])
         nc.sync.dma_start(keep_list[:], koffs)
+        nc.sync.dma_start(out=dz_raw[1][:], in_=dz_rows[:, :, HALF:MERGED])
         nc.sync.dma_start(out=keep_weight[:], in_=wk)
         nc.sync.dma_start(gone_list[:], goffs)
         nc.sync.dma_start(out=gone_weight[:], in_=wg)
+        nc.sync.dma_start(out=w_raw[1][:], in_=w_rows[:, :, HALF:FEATURES])
 
-        windows = [pool.tile([P, TOKENS], F32, name=f"window{n}") for n in range(WINDOWS)]
-        for window, engine in zip(windows, (nc.vector, nc.gpsimd, nc.vector)):
-            engine.memset(window[:].bitcast(I32), 0)
-
+        early, late, whole = slice(0, HALF), slice(HALF, MERGED), slice(0, MERGED)
         dz_codes = pool.tile([P, MERGED], U32, name="dz_codes", align_bytes=64)
         dz_scales = pool.tile([P, MERGED], U8, name="dz_scales", align_bytes=64)
-        for h, round_and_group in enumerate((nc.scalar.copy, nc.vector.tensor_copy)):
-            grouped = pool.tile([P, HALF * LANES], BF16, name=f"dz_grouped{h}", align_bytes=64)
-            round_and_group(
+        nc.vector.memset(dz_codes[:, late], 0)
+        nc.vector.memset(dz_scales[:, late].bitcast(U32), 0)
+        windows = [pool.tile([P, TOKENS], F32, name=f"window{n}") for n in range(WINDOWS)]
+        for window in windows:
+            nc.vector.memset(window[:].bitcast(I32), 0)
+        identity = pool.tile([P, P], F32, name="identity")
+        make_identity(nc, identity[:])
+
+        def round_and_group(copy, raw, name):
+            width = raw.shape[2]
+            grouped = pool.tile([P, width * LANES], BF16, name=name, align_bytes=64)
+            copy(
                 out=grouped[:].rearrange("p (c i j) -> p c j i", i=4, j=LANES),
-                in_=dz_raw[h][:].rearrange("p j (c i) -> p c j i", i=4),
+                in_=raw.rearrange("p j (c i) -> p c j i", i=4),
             )
-            columns = slice(h * HALF, (h + 1) * HALF)
-            nc.vector.quantize_mx(
-                out=dz_codes[:, columns].bitcast(E5M2), scales=dz_scales[:, columns], in_=grouped[:]
-            )
+            return grouped
 
-        first = LANE_ORDER[0]
-        w_codes = [pool.tile([P, P], U32, name=f"w_codes{t}", align_bytes=64) for t in range(LANES)]
-        w_scales = [pool.tile([P, P], U8, name=f"w_scales{t}", align_bytes=64) for t in range(LANES)]
-        per_half = HALF // LANES
-        for h, round_and_group in enumerate((nc.scalar.copy, nc.vector.tensor_copy)):
-            grouped = pool.tile([P, per_half * LANES], BF16, name=f"w_first{h}", align_bytes=64)
-            round_and_group(
-                out=grouped[:].rearrange("p (m j) -> p m j", j=LANES),
-                in_=w_raw[h][:].rearrange("p j (m t) -> p t m j", t=LANES)[:, first],
+        def group_low_lanes(copy, h):
+            grouped = pool.tile([P, P * LANES], BF16, name=f"w_low{h}", align_bytes=64)
+            copy(
+                out=grouped[:].rearrange("p (w e j) -> p w j e", e=2, j=LANES),
+                in_=w_raw[h][:].rearrange("p j (w t) -> p w j t", t=LANES)[:, :, :, 0:2],
             )
-            columns = slice(h * per_half, (h + 1) * per_half)
-            nc.vector.quantize_mx(
-                out=w_codes[first][:, columns].bitcast(E4M3), scales=w_scales[first][:, columns], in_=grouped[:]
-            )
-        w_rest = pool.tile([P, (LANES - 1) * P * LANES], BF16, name="w_rest", align_bytes=64)
-        w_rest_view = w_rest[:].rearrange("p (t h m j) -> p h m j t", t=LANES - 1, h=2, j=LANES)
-        for h in range(2):
+            return grouped
+
+        w_high = pool.tile([P, 2 * P * LANES], BF16, name="w_high", align_bytes=64)
+
+        def group_high_lanes(h):
             nc.scalar.copy(
-                out=w_rest_view[:, h],
-                in_=w_raw[h][:].rearrange("p j (m t) -> p m j t", t=LANES)[:, :, :, 1:LANES],
-            )
-        for t in LANE_ORDER[1:]:
-            nc.vector.quantize_mx(
-                out=w_codes[t][:].bitcast(E4M3),
-                scales=w_scales[t][:],
-                in_=w_rest[:, (t - 1) * P * LANES : t * P * LANES],
+                out=w_high[:].rearrange("p (e h w j) -> p h w j e", e=2, h=2, j=LANES)[:, h],
+                in_=w_raw[h][:].rearrange("p j (w t) -> p w j t", t=LANES)[:, :, :, 2:4],
             )
 
-        acc = {}
-        for t in LANE_ORDER:
-            acc[t] = psum.tile([P, MERGED], F32, name=f"acc{t}")
+        def quantize(dtype, codes, scales, grouped):
+            nc.vector.quantize_mx(out=codes.bitcast(dtype), scales=scales, in_=grouped[:])
+
+        def product(codes, scales, columns, copy, name):
+            acc = psum.tile([P, MERGED], F32, name="acc")
             nc.tensor.matmul_mx(
-                out=acc[t][:],
-                lhsT=w_codes[t][:].bitcast(E4M3),
-                lhsT_scale=w_scales[t][:],
+                out=acc[:],
+                lhsT=codes.bitcast(E4M3),
+                lhsT_scale=scales,
                 rhs=dz_codes[:].bitcast(E5M2),
                 rhs_scale=dz_scales[:],
                 start=True,
                 stop=True,
             )
-
-        def product_in_sbuf(t):
-            u = ring.tile([P, MERGED], F32, name="u")
-            nc.scalar.copy(out=u[:], in_=acc[t][:])
+            u = pool.tile([P, columns.stop - columns.start], F32, name=name, align_bytes=64)
+            copy(out=u[:], in_=acc[:, columns])
             return u
 
-        out_rows = out_0.rearrange("(p t) c -> p t c", t=LANES)
+        def scatter(window, offsets, weight, u, columns):
+            entries = slice(columns.start // 16, columns.stop // 16)
+            nc.vector.tensor_tensor(window[:].indirect(offsets[:, entries]), u[:], weight[:, columns], MULT)
+
+        w_scales = pool.tile([P, FEATURES], U8, name="w_scales", align_bytes=64)
+        first_codes = pool.tile([P, P], U32, name="first_codes", align_bytes=64)
+
+        def quantize_dz(h):
+            for n, copy in enumerate((nc.vector.tensor_copy, nc.scalar.copy)):
+                grouped = round_and_group(copy, dz_raw[h][:, :, n * P : (n + 1) * P], f"dz_grouped{h}{n}")
+                columns = slice(h * HALF + n * P, h * HALF + (n + 1) * P)
+                quantize(E5M2, dz_codes[:, columns], dz_scales[:, columns], grouped)
+
+        quantize_dz(0)
+        quantize(E4M3, first_codes[:], w_scales[:, 0:P], group_low_lanes(nc.vector.tensor_copy, 0))
+        u_early = product(first_codes[:], w_scales[:, 0:P], early, nc.vector.tensor_copy, "u_early")
+        quantize_dz(1)
+        group_high_lanes(0)
+        w_second = group_low_lanes(nc.scalar.copy, 1)
+        group_high_lanes(1)
+        u_late = product(first_codes[:], w_scales[:, 0:P], late, nc.scalar.copy, "w_raw1")
+        scatter(windows[0], keep_list, keep_weight, u_early, early)
+        scatter(windows[0], gone_list, gone_weight, u_early, early)
+        scatter(windows[0], keep_list, keep_weight, u_late, late)
+        later_codes = pool.tile([P, FEATURES - P], U32, name="u_early", align_bytes=64)
+        quantize(E4M3, later_codes[:, 0:P], w_scales[:, P : 2 * P], w_second)
+        quantize(E4M3, later_codes[:, P:], w_scales[:, 2 * P :], w_high)
+        scatter(windows[0], gone_list, gone_weight, u_late, late)
+        products = [None] + [
+            product(
+                later_codes[:, (g - 1) * P : g * P],
+                w_scales[:, g * P : (g + 1) * P],
+                whole,
+                nc.scalar.copy,
+                f"u{g}",
+            )
+            for g in range(1, GROUPS)
+        ]
+
+        out_rows = out_0.rearrange("(w t) c -> w t c", t=LANES)
         grouped_out = [
             pool.tile([P, CHUNK * LANES], BF16, name=f"grouped_out{c}", align_bytes=64) for c in range(CHUNKS)
         ]
+        pairs = [pool.tile([P, BLOCKS, 2, P], BF16, name=f"pairs{c}") for c in range(CHUNKS)]
 
-        def round_into_lane(copy, window, t, c):
-            copy(
-                out=grouped_out[c][:].rearrange("p (c t) -> p t c", t=LANES)[:, t],
-                in_=window[:, c * CHUNK : (c + 1) * CHUNK],
+        def turn(window, h, c):
+            turned = psum.tile([P, BLOCKS, P], F32, name=f"bank{c}")
+            for b in range(BLOCKS):
+                first = c * CHUNK + b * P
+                nc.tensor.transpose(turned[:, b, :], window[:, first : first + P], identity[:])
+            nc.scalar.copy(out=pairs[c][:, :, h, :], in_=turned[:])
+
+        def turn_back(c):
+            back = psum.tile([P, CHUNK], F32, name=f"bank{c}")
+            words = pairs[c][:].rearrange("p b h q -> p (b h q)").bitcast(F32)
+            for b in range(BLOCKS):
+                nc.tensor.transpose(back[:, b * P : (b + 1) * P], words[:, b * P : (b + 1) * P], identity[:])
+            nc.scalar.copy(
+                out=grouped_out[c][:].bitcast(F32).rearrange("p (c u) -> p c u", u=2),
+                in_=back[:].unsqueeze(2).to_broadcast([P, CHUNK, 2]),
             )
 
-        u_keep = product_in_sbuf(LANE_ORDER[0])
-        u_gone = product_in_sbuf(LANE_ORDER[0])
-        u_next = None
-        for n, t in enumerate(LANE_ORDER):
-            window = windows[n % WINDOWS]
-            nc.vector.tensor_tensor(window[:].indirect(keep_list[:]), u_keep[:], keep_weight[:], MULT)
-            if n == 0:
-                u_next = product_in_sbuf(LANE_ORDER[1])
-            nc.vector.tensor_tensor(window[:].indirect(gone_list[:]), u_gone[:], gone_weight[:], MULT)
-            nc.sync.dma_start(out=out_rows[:, t, :], in_=window[:])
-            u_keep = u_gone = u_next
-            for c in range(CHUNKS):
-                on_vector = n == LANES - 1 and c < VECTOR_CHUNKS
-                round_into_lane(nc.vector.tensor_copy if on_vector else nc.scalar.copy, window, t, c)
-                if c == 0 and n + 2 < LANES:
-                    u_next = product_in_sbuf(LANE_ORDER[n + 2])
+        def round_into_lanes(copy, window, t, c):
+            copy(
+                out=grouped_out[c][:].rearrange("p (c t) -> p c t", t=LANES)[:, :, t:LANES],
+                in_=window[:, c * CHUNK : (c + 1) * CHUNK].unsqueeze(2).to_broadcast([P, CHUNK, LANES - t]),
+            )
+
+        for g in range(GROUPS):
+            window = windows[g % WINDOWS]
+            if g > 0:
+                scatter(window, keep_list, keep_weight, products[g], whole)
+                scatter(window, gone_list, gone_weight, products[g], whole)
+            if g < 2:
+                nc.sync.dma_start(out=out_rows[g * 64 : (g + 1) * 64, 0:2, :], in_=window[:])
+                for c in range(CHUNKS):
+                    turn(window, g, c)
+                if g == 1:
+                    for c in range(CHUNKS):
+                        turn_back(c)
+            else:
+                nc.sync.dma_start(out=out_rows[:, g, :], in_=window[:])
+                for c in range(CHUNKS):
+                    on_vector = g == GROUPS - 1 and c < VECTOR_CHUNKS
+                    round_into_lanes(nc.vector.tensor_copy if on_vector else nc.scalar.copy, window, g, c)
 
         out_words = out_1.rearrange("a p c t -> (a p) (c t)").bitcast(I32)
         out_scales = pool.tile([P, CHUNK], U8, name="out_scales", align_bytes=64)

@@ -23,7 +23,8 @@ GROUPS = FEATURES // P
 CHUNK = 512
 CHUNKS = TOKENS // CHUNK
 BLOCKS = CHUNK // P
-VECTOR_CHUNKS = 2
+VECTOR_FIRST = 640
+VECTOR_TOKENS = 1152
 WINDOWS = 2
 
 FLOPS = 2 * 512 * 512 * 512
@@ -57,9 +58,8 @@ def tile_attend_gmerge_pl_kernel(tc, W, dz, wk, wg, koffs, goffs, out_0, out_1, 
         dz_scales = pool.tile([P, MERGED], U8, name="dz_scales", align_bytes=64)
         nc.vector.memset(dz_codes[:, late], 0)
         nc.vector.memset(dz_scales[:, late].bitcast(U32), 0)
-        windows = [pool.tile([P, TOKENS], F32, name=f"window{n}") for n in range(WINDOWS)]
-        for window in windows:
-            nc.vector.memset(window[:].bitcast(I32), 0)
+        windows = [pool.tile([P, TOKENS], F32, name="window0")]
+        nc.vector.memset(windows[0][:].bitcast(I32), 0)
         identity = pool.tile([P, P], F32, name="identity")
         make_identity(nc, identity[:])
 
@@ -123,6 +123,8 @@ def tile_attend_gmerge_pl_kernel(tc, W, dz, wk, wg, koffs, goffs, out_0, out_1, 
         quantize(E4M3, first_codes[:], w_scales[:, 0:P], group_low_lanes(nc.vector.tensor_copy, 0))
         u_early = product(first_codes[:], w_scales[:, 0:P], early, nc.vector.tensor_copy, "u_early")
         quantize_dz(1)
+        windows.append(pool.tile([P, TOKENS], F32, name="dz_grouped11", align_bytes=64))
+        nc.gpsimd.memset(windows[1][:].bitcast(I32), 0)
         group_high_lanes(0)
         w_second = group_low_lanes(nc.scalar.copy, 1)
         group_high_lanes(1)
@@ -146,9 +148,8 @@ def tile_attend_gmerge_pl_kernel(tc, W, dz, wk, wg, koffs, goffs, out_0, out_1, 
         ]
 
         out_rows = out_0.rearrange("(w t) c -> w t c", t=LANES)
-        grouped_out = [
-            pool.tile([P, CHUNK * LANES], BF16, name=f"grouped_out{c}", align_bytes=64) for c in range(CHUNKS)
-        ]
+        grouped_out = pool.tile([P, TOKENS * LANES], BF16, name="grouped_out", align_bytes=64)
+        chunk_values = [grouped_out[:, c * CHUNK * LANES : (c + 1) * CHUNK * LANES] for c in range(CHUNKS)]
         pairs = [pool.tile([P, BLOCKS, 2, P], BF16, name=f"pairs{c}") for c in range(CHUNKS)]
 
         def turn(window, h, c):
@@ -164,14 +165,14 @@ def tile_attend_gmerge_pl_kernel(tc, W, dz, wk, wg, koffs, goffs, out_0, out_1, 
             for b in range(BLOCKS):
                 nc.tensor.transpose(back[:, b * P : (b + 1) * P], words[:, b * P : (b + 1) * P], identity[:])
             nc.scalar.copy(
-                out=grouped_out[c][:].bitcast(F32).rearrange("p (c u) -> p c u", u=2),
+                out=chunk_values[c].bitcast(F32).rearrange("p (c u) -> p c u", u=2),
                 in_=back[:].unsqueeze(2).to_broadcast([P, CHUNK, 2]),
             )
 
-        def round_into_lanes(copy, window, t, c):
+        def round_into_lanes(copy, window, t, first, stop):
             copy(
-                out=grouped_out[c][:].rearrange("p (c t) -> p c t", t=LANES)[:, :, t:LANES],
-                in_=window[:, c * CHUNK : (c + 1) * CHUNK].unsqueeze(2).to_broadcast([P, CHUNK, LANES - t]),
+                out=grouped_out[:].rearrange("p (c t) -> p c t", t=LANES)[:, first:stop, t:LANES],
+                in_=window[:, first:stop].unsqueeze(2).to_broadcast([P, stop - first, LANES - t]),
             )
 
         for g in range(GROUPS):
@@ -188,22 +189,27 @@ def tile_attend_gmerge_pl_kernel(tc, W, dz, wk, wg, koffs, goffs, out_0, out_1, 
                         turn_back(c)
             else:
                 nc.sync.dma_start(out=out_rows[:, g, :], in_=window[:])
-                for c in range(CHUNKS):
-                    on_vector = g == GROUPS - 1 and c < VECTOR_CHUNKS
-                    round_into_lanes(nc.vector.tensor_copy if on_vector else nc.scalar.copy, window, g, c)
+                if g == 2:
+                    for c in (0, 2, 1, 3):
+                        round_into_lanes(nc.scalar.copy, window, g, c * CHUNK, (c + 1) * CHUNK)
+                else:
+                    round_into_lanes(nc.vector.tensor_copy, window, g, 0, VECTOR_FIRST)
+                    round_into_lanes(nc.vector.tensor_copy, window, g, VECTOR_FIRST, VECTOR_TOKENS)
+                    round_into_lanes(nc.scalar.copy, window, g, VECTOR_TOKENS, 3 * CHUNK)
+                    round_into_lanes(nc.scalar.copy, window, g, 3 * CHUNK, TOKENS)
 
         out_words = out_1.rearrange("a p c t -> (a p) (c t)").bitcast(I32)
-        out_scales = pool.tile([P, CHUNK], U8, name="out_scales", align_bytes=64)
+        out_scales = pool.tile([P, 2 * CHUNK], U8, name="out_scales", align_bytes=64)
         for c in range(CHUNKS):
             codes = pool.tile([P, CHUNK], U32, name=f"out_codes{c}", align_bytes=64)
             nc.vector.quantize_mx(
-                out=codes[:].bitcast(E4M3), scales=out_scales[4 * c : P, :], in_=grouped_out[c][:]
+                out=codes[:].bitcast(E4M3), scales=out_scales[4 * (c // 2) : P, (c % 2) * CHUNK : (c % 2 + 1) * CHUNK], in_=chunk_values[c]
             )
             nc.sync.dma_start(out=out_words[:, c * CHUNK : (c + 1) * CHUNK], in_=codes[:].bitcast(I32))
-        scale_rows = out_2.rearrange("a b c -> (a b) c").bitcast(I32).rearrange("b (c w) -> c b w", c=CHUNKS)
+        scale_rows = out_2.rearrange("a b c -> (a b) c").bitcast(I32).rearrange("b (c w) -> c b w", c=2)
         for q in range(4):
             queue = nc.sync if q % 2 == 0 else nc.scalar
             queue.dma_start(
                 out=scale_rows[:, 4 * q : 4 * q + 4, :],
-                in_=out_scales[32 * q : 32 * q + 16, :].bitcast(I32),
+                in_=out_scales[32 * q : 32 * q + 8, :].bitcast(I32),
             )

@@ -49,9 +49,9 @@ def tile_attend_gmerge_pl_kernel(tc, W, dz, wk, wg, koffs, goffs, out_0, out_1, 
         nc.sync.dma_start(keep_list[:], koffs)
         nc.sync.dma_start(out=dz_raw[1][:], in_=dz_rows[:, :, HALF:MERGED])
         nc.sync.dma_start(out=keep_weight[:], in_=wk)
+        nc.sync.dma_start(out=w_raw[1][:], in_=w_rows[:, :, HALF:FEATURES])
         nc.sync.dma_start(gone_list[:], goffs)
         nc.sync.dma_start(out=gone_weight[:], in_=wg)
-        nc.sync.dma_start(out=w_raw[1][:], in_=w_rows[:, :, HALF:FEATURES])
 
         early, late, whole = slice(0, HALF), slice(HALF, MERGED), slice(0, MERGED)
         dz_codes = pool.tile([P, MERGED], U32, name="dz_codes", align_bytes=64)
@@ -72,12 +72,13 @@ def tile_attend_gmerge_pl_kernel(tc, W, dz, wk, wg, koffs, goffs, out_0, out_1, 
             )
             return grouped
 
-        def group_low_lanes(copy, h):
+        def group_low_lanes(shares, h):
             grouped = pool.tile([P, P * LANES], BF16, name=f"w_low{h}", align_bytes=64)
-            copy(
-                out=grouped[:].rearrange("p (w e j) -> p w j e", e=2, j=LANES),
-                in_=w_raw[h][:].rearrange("p j (w t) -> p w j t", t=LANES)[:, :, :, 0:2],
-            )
+            for copy, words in shares:
+                copy(
+                    out=grouped[:].rearrange("p (w e j) -> p w j e", e=2, j=LANES)[:, words],
+                    in_=w_raw[h][:].rearrange("p j (w t) -> p w j t", t=LANES)[:, words, :, 0:2],
+                )
             return grouped
 
         w_high = pool.tile([P, 2 * P * LANES], BF16, name="w_high", align_bytes=64)
@@ -91,8 +92,8 @@ def tile_attend_gmerge_pl_kernel(tc, W, dz, wk, wg, koffs, goffs, out_0, out_1, 
         def quantize(dtype, codes, scales, grouped):
             nc.vector.quantize_mx(out=codes.bitcast(dtype), scales=scales, in_=grouped[:])
 
-        def product(codes, scales, columns, copy, name):
-            acc = psum.tile([P, MERGED], F32, name="acc")
+        def product(codes, scales):
+            acc = psum.tile([P, MERGED], F32, name="acc", bufs=2)
             nc.tensor.matmul_mx(
                 out=acc[:],
                 lhsT=codes.bitcast(E4M3),
@@ -102,6 +103,9 @@ def tile_attend_gmerge_pl_kernel(tc, W, dz, wk, wg, koffs, goffs, out_0, out_1, 
                 start=True,
                 stop=True,
             )
+            return acc
+
+        def to_sbuf(copy, acc, columns, name):
             u = pool.tile([P, columns.stop - columns.start], F32, name=name, align_bytes=64)
             copy(out=u[:], in_=acc[:, columns])
             return u
@@ -113,39 +117,38 @@ def tile_attend_gmerge_pl_kernel(tc, W, dz, wk, wg, koffs, goffs, out_0, out_1, 
         w_scales = pool.tile([P, FEATURES], U8, name="w_scales", align_bytes=64)
         first_codes = pool.tile([P, P], U32, name="first_codes", align_bytes=64)
 
-        def quantize_dz(h):
-            for n, copy in enumerate((nc.vector.tensor_copy, nc.scalar.copy)):
-                grouped = round_and_group(copy, dz_raw[h][:, :, n * P : (n + 1) * P], f"dz_grouped{h}{n}")
-                columns = slice(h * HALF + n * P, h * HALF + (n + 1) * P)
-                quantize(E5M2, dz_codes[:, columns], dz_scales[:, columns], grouped)
-
-        quantize_dz(0)
-        quantize(E4M3, first_codes[:], w_scales[:, 0:P], group_low_lanes(nc.vector.tensor_copy, 0))
-        u_early = product(first_codes[:], w_scales[:, 0:P], early, nc.vector.tensor_copy, "u_early")
-        quantize_dz(1)
-        windows.append(pool.tile([P, TOKENS], F32, name="dz_grouped11", align_bytes=64))
+        for n, copy in enumerate((nc.vector.tensor_copy, nc.scalar.copy)):
+            columns = slice(n * P, (n + 1) * P)
+            grouped = round_and_group(copy, dz_raw[0][:, :, columns], f"dz_early{n}")
+            quantize(E5M2, dz_codes[:, columns], dz_scales[:, columns], grouped)
+        quantize(E4M3, first_codes[:], w_scales[:, 0:P], group_low_lanes(((nc.vector.tensor_copy, slice(0, 40)), (nc.scalar.copy, slice(40, 64))), 0))
+        windows.append(pool.tile([P, TOKENS], F32, name="w_low0", align_bytes=64))
         nc.gpsimd.memset(windows[1][:].bitcast(I32), 0)
+        acc = product(first_codes[:], w_scales[:, 0:P])
+        u_early = to_sbuf(nc.vector.tensor_copy, acc, early, "u_early")
         group_high_lanes(0)
-        w_second = group_low_lanes(nc.scalar.copy, 1)
+        quantize(E5M2, dz_codes[:, late], dz_scales[:, late], round_and_group(nc.scalar.copy, dz_raw[1][:], "dz_late"))
+        w_second = group_low_lanes(((nc.scalar.copy, slice(0, 64)),), 1)
         group_high_lanes(1)
-        u_late = product(first_codes[:], w_scales[:, 0:P], late, nc.scalar.copy, "w_raw1")
+        acc_late = product(first_codes[:], w_scales[:, 0:P])
+        late_keep = to_sbuf(nc.scalar.copy, acc_late, late, "w_raw1")
         scatter(windows[0], keep_list, keep_weight, u_early, early)
         scatter(windows[0], gone_list, gone_weight, u_early, early)
-        scatter(windows[0], keep_list, keep_weight, u_late, late)
-        later_codes = pool.tile([P, FEATURES - P], U32, name="u_early", align_bytes=64)
-        quantize(E4M3, later_codes[:, 0:P], w_scales[:, P : 2 * P], w_second)
-        quantize(E4M3, later_codes[:, P:], w_scales[:, 2 * P :], w_high)
-        scatter(windows[0], gone_list, gone_weight, u_late, late)
-        products = [None] + [
-            product(
-                later_codes[:, (g - 1) * P : g * P],
-                w_scales[:, g * P : (g + 1) * P],
-                whole,
-                nc.scalar.copy,
-                f"u{g}",
-            )
-            for g in range(1, GROUPS)
-        ]
+        second_codes = pool.tile([P, P], U32, name="u_early", align_bytes=64)
+        quantize(E4M3, second_codes[:], w_scales[:, P : 2 * P], w_second)
+        high_codes = pool.tile([P, 2 * P], U32, name="high_codes", align_bytes=64)
+        quantize(E4M3, high_codes[:], w_scales[:, 2 * P :], w_high)
+        windows.append(pool.tile([P, TOKENS], F32, name="w_high", align_bytes=64))
+        nc.gpsimd.memset(windows[2][:].bitcast(I32), 0)
+        scatter(windows[0], keep_list, keep_weight, late_keep, late)
+        u1 = to_sbuf(nc.scalar.copy, product(second_codes[:], w_scales[:, P : 2 * P]), whole, "u1")
+        late_gone = to_sbuf(nc.scalar.copy, acc_late, late, "u_early")
+        scatter(windows[1], keep_list, keep_weight, u1, whole)
+        scatter(windows[0], gone_list, gone_weight, late_gone, late)
+        scatter(windows[1], gone_list, gone_weight, u1, whole)
+        u2 = to_sbuf(nc.scalar.copy, product(high_codes[:, 0:P], w_scales[:, 2 * P : 3 * P]), whole, "u_early")
+        u3 = to_sbuf(nc.scalar.copy, product(high_codes[:, P:], w_scales[:, 3 * P :]), whole, "u3")
+        products = [None, u1, u2, u3]
 
         out_rows = out_0.rearrange("(w t) c -> w t c", t=LANES)
         grouped_out = pool.tile([P, TOKENS * LANES], BF16, name="grouped_out", align_bytes=64)
@@ -176,8 +179,8 @@ def tile_attend_gmerge_pl_kernel(tc, W, dz, wk, wg, koffs, goffs, out_0, out_1, 
             )
 
         for g in range(GROUPS):
-            window = windows[g % WINDOWS]
-            if g > 0:
+            window = windows[(0, 1, 2, 1)[g]]
+            if g > 1:
                 scatter(window, keep_list, keep_weight, products[g], whole)
                 scatter(window, gone_list, gone_weight, products[g], whole)
             if g < 2:

@@ -47,8 +47,8 @@ def tile_attend_gmerge_pl_kernel(tc, W, dz, wk, wg, koffs, goffs, out_0, out_1, 
         nc.sync.dma_start(out=dz_raw[0][:], in_=dz_rows[:, :, 0:HALF])
         nc.sync.dma_start(out=w_raw[0][:], in_=w_rows[:, :, 0:HALF])
         nc.sync.dma_start(keep_list[:], koffs)
-        nc.sync.dma_start(out=dz_raw[1][:], in_=dz_rows[:, :, HALF:MERGED])
         nc.sync.dma_start(out=keep_weight[:], in_=wk)
+        nc.sync.dma_start(out=dz_raw[1][:], in_=dz_rows[:, :, HALF:MERGED])
         nc.sync.dma_start(out=w_raw[1][:], in_=w_rows[:, :, HALF:FEATURES])
         nc.sync.dma_start(gone_list[:], goffs)
         nc.sync.dma_start(out=gone_weight[:], in_=wg)

@@ -25,7 +25,8 @@ CHUNKS = TOKENS // CHUNK
 BLOCKS = CHUNK // P
 VECTOR_FIRST = 640
 VECTOR_TOKENS = 1152
-WINDOWS = 2
+FILL = 192
+FILL_CHUNK = 2
 
 FLOPS = 2 * 512 * 512 * 512
 
@@ -182,6 +183,8 @@ def tile_attend_gmerge_pl_kernel(tc, W, dz, wk, wg, koffs, goffs, out_0, out_1, 
             window = windows[(0, 1, 2, 1)[g]]
             if g > 1:
                 scatter(window, keep_list, keep_weight, products[g], whole)
+                if g == 3:
+                    round_into_lanes(nc.vector.tensor_copy, windows[2], 2, FILL_CHUNK * CHUNK, FILL_CHUNK * CHUNK + FILL)
                 scatter(window, gone_list, gone_weight, products[g], whole)
             if g < 2:
                 nc.sync.dma_start(out=out_rows[g * 64 : (g + 1) * 64, 0:2, :], in_=window[:])
@@ -194,7 +197,7 @@ def tile_attend_gmerge_pl_kernel(tc, W, dz, wk, wg, koffs, goffs, out_0, out_1, 
                 nc.sync.dma_start(out=out_rows[:, g, :], in_=window[:])
                 if g == 2:
                     for c in (0, 2, 1, 3):
-                        round_into_lanes(nc.scalar.copy, window, g, c * CHUNK, (c + 1) * CHUNK)
+                        round_into_lanes(nc.scalar.copy, window, g, c * CHUNK + FILL * (c == FILL_CHUNK), (c + 1) * CHUNK)
                 else:
                     round_into_lanes(nc.vector.tensor_copy, window, g, 0, VECTOR_FIRST)
                     round_into_lanes(nc.vector.tensor_copy, window, g, VECTOR_FIRST, VECTOR_TOKENS)

@@ -24,7 +24,7 @@ CHUNK = 512
 CHUNKS = TOKENS // CHUNK
 BLOCKS = CHUNK // P
 VECTOR_FIRST = 640
-VECTOR_TOKENS = 1152
+VECTOR_TOKENS = 960
 FILL = 192
 FILL_CHUNK = 2
 
@@ -197,21 +197,39 @@ def tile_attend_gmerge_pl_kernel(tc, W, dz, wk, wg, koffs, goffs, out_0, out_1, 
                 nc.sync.dma_start(out=out_rows[:, g, :], in_=window[:])
                 if g == 2:
                     for c in (0, 2, 1, 3):
-                        round_into_lanes(nc.scalar.copy, window, g, c * CHUNK + FILL * (c == FILL_CHUNK), (c + 1) * CHUNK)
+                        round_into_lanes(nc.scalar.copy, window, g, c * CHUNK + FILL * (c >= FILL_CHUNK), (c + 1) * CHUNK)
                 else:
-                    round_into_lanes(nc.vector.tensor_copy, window, g, 0, VECTOR_FIRST)
-                    round_into_lanes(nc.vector.tensor_copy, window, g, VECTOR_FIRST, VECTOR_TOKENS)
-                    round_into_lanes(nc.scalar.copy, window, g, VECTOR_TOKENS, 3 * CHUNK)
-                    round_into_lanes(nc.scalar.copy, window, g, 3 * CHUNK, TOKENS)
+                    last = window
 
         out_words = out_1.rearrange("a p c t -> (a p) (c t)").bitcast(I32)
         out_scales = pool.tile([P, 2 * CHUNK], U8, name="out_scales", align_bytes=64)
-        for c in range(CHUNKS):
-            codes = pool.tile([P, CHUNK], U32, name=f"out_codes{c}", align_bytes=64)
+        out_codes = [pool.tile([P, CHUNK], U32, name=f"out_codes{c}", align_bytes=64) for c in range(CHUNKS)]
+
+        def quantize_tokens(first, stop):
+            c, at = divmod(first, CHUNK)
+            column = (c % 2) * CHUNK + at
             nc.vector.quantize_mx(
-                out=codes[:].bitcast(E4M3), scales=out_scales[4 * (c // 2) : P, (c % 2) * CHUNK : (c % 2 + 1) * CHUNK], in_=chunk_values[c]
+                out=out_codes[c][:, at : at + stop - first].bitcast(E4M3),
+                scales=out_scales[4 * (c // 2) : P, column : column + stop - first],
+                in_=grouped_out[:, first * LANES : stop * LANES],
             )
-            nc.sync.dma_start(out=out_words[:, c * CHUNK : (c + 1) * CHUNK], in_=codes[:].bitcast(I32))
+
+        def store_chunk(c):
+            nc.sync.dma_start(out=out_words[:, c * CHUNK : (c + 1) * CHUNK], in_=out_codes[c][:].bitcast(I32))
+
+        round_into_lanes(nc.vector.tensor_copy, windows[2], 2, 3 * CHUNK, 3 * CHUNK + FILL)
+        round_into_lanes(nc.vector.tensor_copy, last, 3, 0, VECTOR_FIRST)
+        round_into_lanes(nc.vector.tensor_copy, last, 3, VECTOR_FIRST, VECTOR_TOKENS)
+        round_into_lanes(nc.scalar.copy, last, 3, VECTOR_TOKENS, 2 * CHUNK)
+        round_into_lanes(nc.scalar.copy, last, 3, 2 * CHUNK, 3 * CHUNK)
+        round_into_lanes(nc.scalar.copy, last, 3, 3 * CHUNK, 3 * CHUNK + HALF)
+        round_into_lanes(nc.scalar.copy, last, 3, 3 * CHUNK + HALF, TOKENS)
+        for c in range(CHUNKS - 1):
+            quantize_tokens(c * CHUNK, (c + 1) * CHUNK)
+            store_chunk(c)
+        quantize_tokens(3 * CHUNK, 3 * CHUNK + HALF)
+        quantize_tokens(3 * CHUNK + HALF, TOKENS)
+        store_chunk(3)
         scale_rows = out_2.rearrange("a b c -> (a b) c").bitcast(I32).rearrange("b (c w) -> c b w", c=2)
         for q in range(4):
             queue = nc.sync if q % 2 == 0 else nc.scalar

@@ -24,7 +24,7 @@ CHUNK = 512
 CHUNKS = TOKENS // CHUNK
 BLOCKS = CHUNK // P
 VECTOR_FIRST = 640
-VECTOR_TOKENS = 960
+VECTOR_TOKENS = 1152
 FILL = 192
 FILL_CHUNK = 2
 
@@ -109,11 +109,11 @@ def tile_attend_gmerge_pl_kernel(tc, W, dz, wk, wg, koffs, goffs, out_0, out_1, 
         def to_sbuf(copy, acc, columns, name):
             u = pool.tile([P, columns.stop - columns.start], F32, name=name, align_bytes=64)
             copy(out=u[:], in_=acc[:, columns])
-            return u
+            return u[:]
 
         def scatter(window, offsets, weight, u, columns):
             entries = slice(columns.start // 16, columns.stop // 16)
-            nc.vector.tensor_tensor(window[:].indirect(offsets[:, entries]), u[:], weight[:, columns], MULT)
+            nc.vector.tensor_tensor(window[:].indirect(offsets[:, entries]), u, weight[:, columns], MULT)
 
         w_scales = pool.tile([P, FEATURES], U8, name="w_scales", align_bytes=64)
         first_codes = pool.tile([P, P], U32, name="first_codes", align_bytes=64)
@@ -139,9 +139,12 @@ def tile_attend_gmerge_pl_kernel(tc, W, dz, wk, wg, koffs, goffs, out_0, out_1, 
         quantize(E4M3, second_codes[:], w_scales[:, P : 2 * P], w_second)
         high_codes = pool.tile([P, 2 * P], U32, name="high_codes", align_bytes=64)
         quantize(E4M3, high_codes[:], w_scales[:, 2 * P :], w_high)
-        windows.append(pool.tile([P, TOKENS], F32, name="w_high", align_bytes=64))
-        nc.gpsimd.memset(windows[2][:].bitcast(I32), 0)
+        last = pool.tile([P, TOKENS], F32, name="w_high", align_bytes=64)
+        nc.gpsimd.memset(last[:, 0 : 3 * CHUNK].bitcast(I32), 0)
         scatter(windows[0], keep_list, keep_weight, late_keep, late)
+        windows.append(pool.tile([P, TOKENS], F32, name="w_raw1", align_bytes=64))
+        nc.gpsimd.memset(windows[2][:].bitcast(I32), 0)
+        nc.gpsimd.memset(last[:, 3 * CHUNK :].bitcast(I32), 0)
         u1 = to_sbuf(nc.scalar.copy, product(second_codes[:], w_scales[:, P : 2 * P]), whole, "u1")
         late_gone = to_sbuf(nc.scalar.copy, acc_late, late, "u_early")
         scatter(windows[1], keep_list, keep_weight, u1, whole)
@@ -149,7 +152,6 @@ def tile_attend_gmerge_pl_kernel(tc, W, dz, wk, wg, koffs, goffs, out_0, out_1, 
         scatter(windows[1], gone_list, gone_weight, u1, whole)
         u2 = to_sbuf(nc.scalar.copy, product(high_codes[:, 0:P], w_scales[:, 2 * P : 3 * P]), whole, "u_early")
         u3 = to_sbuf(nc.scalar.copy, product(high_codes[:, P:], w_scales[:, 3 * P :]), whole, "u3")
-        products = [None, u1, u2, u3]
 
         out_rows = out_0.rearrange("(w t) c -> w t c", t=LANES)
         grouped_out = pool.tile([P, TOKENS * LANES], BF16, name="grouped_out", align_bytes=64)
@@ -168,9 +170,15 @@ def tile_attend_gmerge_pl_kernel(tc, W, dz, wk, wg, koffs, goffs, out_0, out_1, 
             words = pairs[c][:].rearrange("p b h q -> p (b h q)").bitcast(F32)
             for b in range(BLOCKS):
                 nc.tensor.transpose(back[:, b * P : (b + 1) * P], words[:, b * P : (b + 1) * P], identity[:])
+            first = FILL * (c == FILL_CHUNK)
+            if first:
+                nc.scalar.copy(
+                    out=chunk_values[c].rearrange("p (c t) -> p c t", t=LANES)[:, 0:first, 0:2],
+                    in_=back[:, 0:first].bitcast(BF16).rearrange("p (c t) -> p c t", t=2),
+                )
             nc.scalar.copy(
-                out=chunk_values[c].bitcast(F32).rearrange("p (c u) -> p c u", u=2),
-                in_=back[:].unsqueeze(2).to_broadcast([P, CHUNK, 2]),
+                out=chunk_values[c].bitcast(F32).rearrange("p (c u) -> p c u", u=2)[:, first:],
+                in_=back[:, first:].unsqueeze(2).to_broadcast([P, CHUNK - first, 2]),
             )
 
         def round_into_lanes(copy, window, t, first, stop):
@@ -179,27 +187,22 @@ def tile_attend_gmerge_pl_kernel(tc, W, dz, wk, wg, koffs, goffs, out_0, out_1, 
                 in_=window[:, first:stop].unsqueeze(2).to_broadcast([P, stop - first, LANES - t]),
             )
 
-        for g in range(GROUPS):
-            window = windows[(0, 1, 2, 1)[g]]
-            if g > 1:
-                scatter(window, keep_list, keep_weight, products[g], whole)
-                if g == 3:
-                    round_into_lanes(nc.vector.tensor_copy, windows[2], 2, FILL_CHUNK * CHUNK, FILL_CHUNK * CHUNK + FILL)
-                scatter(window, gone_list, gone_weight, products[g], whole)
-            if g < 2:
-                nc.sync.dma_start(out=out_rows[g * 64 : (g + 1) * 64, 0:2, :], in_=window[:])
-                for c in range(CHUNKS):
-                    turn(window, g, c)
-                if g == 1:
-                    for c in range(CHUNKS):
-                        turn_back(c)
-            else:
-                nc.sync.dma_start(out=out_rows[:, g, :], in_=window[:])
-                if g == 2:
-                    for c in (0, 2, 1, 3):
-                        round_into_lanes(nc.scalar.copy, window, g, c * CHUNK + FILL * (c >= FILL_CHUNK), (c + 1) * CHUNK)
-                else:
-                    last = window
+        for g in range(2):
+            nc.sync.dma_start(out=out_rows[g * 64 : (g + 1) * 64, 0:2, :], in_=windows[g][:])
+            for c in range(CHUNKS):
+                turn(windows[g], g, c)
+        for c in range(CHUNKS):
+            turn_back(c)
+        scatter(windows[2], keep_list, keep_weight, u2, whole)
+        scatter(last, keep_list, keep_weight, u3[:, early], early)
+        scatter(windows[2], gone_list, gone_weight, u2, whole)
+        nc.sync.dma_start(out=out_rows[:, 2, :], in_=windows[2][:])
+        for c in (0, 2, 1, 3):
+            round_into_lanes(nc.scalar.copy, windows[2], 2, c * CHUNK + FILL * (c >= FILL_CHUNK), (c + 1) * CHUNK)
+        scatter(last, keep_list, keep_weight, u3[:, late], late)
+        round_into_lanes(nc.vector.tensor_copy, windows[2], 2, FILL_CHUNK * CHUNK, FILL_CHUNK * CHUNK + FILL)
+        scatter(last, gone_list, gone_weight, u3, whole)
+        nc.sync.dma_start(out=out_rows[:, 3, :], in_=last[:])
 
         out_words = out_1.rearrange("a p c t -> (a p) (c t)").bitcast(I32)
         out_scales = pool.tile([P, 2 * CHUNK], U8, name="out_scales", align_bytes=64)
@@ -220,8 +223,7 @@ def tile_attend_gmerge_pl_kernel(tc, W, dz, wk, wg, koffs, goffs, out_0, out_1, 
         round_into_lanes(nc.vector.tensor_copy, windows[2], 2, 3 * CHUNK, 3 * CHUNK + FILL)
         round_into_lanes(nc.vector.tensor_copy, last, 3, 0, VECTOR_FIRST)
         round_into_lanes(nc.vector.tensor_copy, last, 3, VECTOR_FIRST, VECTOR_TOKENS)
-        round_into_lanes(nc.scalar.copy, last, 3, VECTOR_TOKENS, 2 * CHUNK)
-        round_into_lanes(nc.scalar.copy, last, 3, 2 * CHUNK, 3 * CHUNK)
+        round_into_lanes(nc.scalar.copy, last, 3, VECTOR_TOKENS, 3 * CHUNK)
         round_into_lanes(nc.scalar.copy, last, 3, 3 * CHUNK, 3 * CHUNK + HALF)
         round_into_lanes(nc.scalar.copy, last, 3, 3 * CHUNK + HALF, TOKENS)
         for c in range(CHUNKS - 1):

@@ -40,7 +40,6 @@ def tile_attend_gmerge_pl_kernel(tc, W, dz, wk, wg, koffs, goffs, out_0, out_1, 
         keep_list = pool.tile([P, MERGED // 16], U16, name="keep_list")
         gone_list = pool.tile([P, MERGED // 16], U16, name="gone_list")
         keep_weight = pool.tile([P, MERGED], F32, name="keep_weight")
-        gone_weight = pool.tile([P, MERGED], F32, name="gone_weight")
         dz_rows = dz.rearrange("(p j) i -> p j i", j=LANES)
         w_rows = W.rearrange("(p j) d -> p j d", j=LANES)
         dz_raw = [pool.tile([P, LANES, HALF], F32, name=f"dz_raw{h}") for h in range(2)]
@@ -48,30 +47,31 @@ def tile_attend_gmerge_pl_kernel(tc, W, dz, wk, wg, koffs, goffs, out_0, out_1, 
         nc.sync.dma_start(out=dz_raw[0][:], in_=dz_rows[:, :, 0:HALF])
         nc.sync.dma_start(out=w_raw[0][:], in_=w_rows[:, :, 0:HALF])
         nc.sync.dma_start(keep_list[:], koffs)
-        nc.sync.dma_start(out=keep_weight[:], in_=wk)
         nc.sync.dma_start(out=dz_raw[1][:], in_=dz_rows[:, :, HALF:MERGED])
+        nc.sync.dma_start(out=keep_weight[:], in_=wk)
         nc.sync.dma_start(out=w_raw[1][:], in_=w_rows[:, :, HALF:FEATURES])
         nc.sync.dma_start(gone_list[:], goffs)
-        nc.sync.dma_start(out=gone_weight[:], in_=wg)
 
         early, late, whole = slice(0, HALF), slice(HALF, MERGED), slice(0, MERGED)
         dz_codes = pool.tile([P, MERGED], U32, name="dz_codes", align_bytes=64)
         dz_scales = pool.tile([P, MERGED], U8, name="dz_scales", align_bytes=64)
-        nc.vector.memset(dz_codes[:, late], 0)
-        nc.vector.memset(dz_scales[:, late].bitcast(U32), 0)
-        windows = [pool.tile([P, TOKENS], F32, name="window0")]
-        nc.vector.memset(windows[0][:].bitcast(I32), 0)
+        nc.vector.memset(dz_codes[:, HALF - 1 :], 0)
+        nc.vector.memset(dz_scales[:, HALF - 4 :].bitcast(U32), 0)
+        windows = [pool.tile([P, TOKENS], F32, name=f"window{g}") for g in range(2)]
+        nc.vector.memset(windows[0][:, 0 : 2 * CHUNK - 1].bitcast(I32), 0)
+        nc.vector.memset(windows[0][:, 2 * CHUNK - 1 :].bitcast(I32), 0)
         identity = pool.tile([P, P], F32, name="identity")
         make_identity(nc, identity[:])
+        nc.gpsimd.memset(windows[1][:].bitcast(I32), 0)
 
-        def round_and_group(copy, raw, name):
-            width = raw.shape[2]
-            grouped = pool.tile([P, width * LANES], BF16, name=name, align_bytes=64)
-            copy(
-                out=grouped[:].rearrange("p (c i j) -> p c j i", i=4, j=LANES),
-                in_=raw.rearrange("p j (c i) -> p c j i", i=4),
-            )
-            return grouped
+        def round_and_group(shares, raw, name):
+            grouped = pool.tile([P, raw.shape[2] * LANES], BF16, name=name, align_bytes=64)
+            for copy, quads in shares:
+                copy(
+                    out=grouped[:].rearrange("p (c i j) -> p c j i", i=4, j=LANES)[:, quads],
+                    in_=raw.rearrange("p j (c i) -> p c j i", i=4)[:, quads],
+                )
+            return grouped[:]
 
         def group_low_lanes(shares, h):
             grouped = pool.tile([P, P * LANES], BF16, name=f"w_low{h}", align_bytes=64)
@@ -80,21 +80,21 @@ def tile_attend_gmerge_pl_kernel(tc, W, dz, wk, wg, koffs, goffs, out_0, out_1, 
                     out=grouped[:].rearrange("p (w e j) -> p w j e", e=2, j=LANES)[:, words],
                     in_=w_raw[h][:].rearrange("p j (w t) -> p w j t", t=LANES)[:, words, :, 0:2],
                 )
-            return grouped
+            return grouped[:]
 
-        w_high = pool.tile([P, 2 * P * LANES], BF16, name="w_high", align_bytes=64)
+        w_high = [pool.tile([P, P * LANES], BF16, name=f"w_high{h}", align_bytes=64) for h in range(2)]
 
         def group_high_lanes(h):
             nc.scalar.copy(
-                out=w_high[:].rearrange("p (e h w j) -> p h w j e", e=2, h=2, j=LANES)[:, h],
+                out=w_high[h][:].rearrange("p (e w j) -> p w j e", e=2, j=LANES),
                 in_=w_raw[h][:].rearrange("p j (w t) -> p w j t", t=LANES)[:, :, :, 2:4],
             )
 
         def quantize(dtype, codes, scales, grouped):
-            nc.vector.quantize_mx(out=codes.bitcast(dtype), scales=scales, in_=grouped[:])
+            nc.vector.quantize_mx(out=codes.bitcast(dtype), scales=scales, in_=grouped)
 
-        def product(codes, scales):
-            acc = psum.tile([P, MERGED], F32, name="acc", bufs=2)
+        def product(codes, scales, bank):
+            acc = psum.tile([P, MERGED], F32, name=bank)
             nc.tensor.matmul_mx(
                 out=acc[:],
                 lhsT=codes.bitcast(E4M3),
@@ -118,40 +118,51 @@ def tile_attend_gmerge_pl_kernel(tc, W, dz, wk, wg, koffs, goffs, out_0, out_1, 
         w_scales = pool.tile([P, FEATURES], U8, name="w_scales", align_bytes=64)
         first_codes = pool.tile([P, P], U32, name="first_codes", align_bytes=64)
 
+        high_codes = pool.tile([P, 2 * P], U32, name="high_codes", align_bytes=64)
+
+        def quantize_high_lanes(h):
+            for e in range(2):
+                first = e * P + h * 64
+                quantize(E4M3, high_codes[:, first : first + 64], w_scales[:, 2 * P + first : 2 * P + first + 64], w_high[h][:, e * HALF : (e + 1) * HALF])
+
         for n, copy in enumerate((nc.vector.tensor_copy, nc.scalar.copy)):
             columns = slice(n * P, (n + 1) * P)
-            grouped = round_and_group(copy, dz_raw[0][:, :, columns], f"dz_early{n}")
+            grouped = round_and_group(((copy, slice(0, 32)),), dz_raw[0][:, :, columns], f"dz_early{n}")
             quantize(E5M2, dz_codes[:, columns], dz_scales[:, columns], grouped)
         quantize(E4M3, first_codes[:], w_scales[:, 0:P], group_low_lanes(((nc.vector.tensor_copy, slice(0, 40)), (nc.scalar.copy, slice(40, 64))), 0))
-        windows.append(pool.tile([P, TOKENS], F32, name="w_low0", align_bytes=64))
-        nc.gpsimd.memset(windows[1][:].bitcast(I32), 0)
-        acc = product(first_codes[:], w_scales[:, 0:P])
+        acc = product(first_codes[:], w_scales[:, 0:P], "acc0")
         u_early = to_sbuf(nc.vector.tensor_copy, acc, early, "u_early")
         group_high_lanes(0)
-        quantize(E5M2, dz_codes[:, late], dz_scales[:, late], round_and_group(nc.scalar.copy, dz_raw[1][:], "dz_late"))
+        dz_late = round_and_group(((nc.vector.tensor_copy, slice(0, 40)), (nc.scalar.copy, slice(40, 64))), dz_raw[1][:], "dz_late")
+        gone_weight = pool.tile([P, MERGED], F32, name="dz_raw1")
+        nc.sync.dma_start(out=gone_weight[:], in_=wg)
+        quantize_high_lanes(0)
+        quantize(E5M2, dz_codes[:, late], dz_scales[:, late], dz_late)
         w_second = group_low_lanes(((nc.scalar.copy, slice(0, 64)),), 1)
         group_high_lanes(1)
-        acc_late = product(first_codes[:], w_scales[:, 0:P])
-        late_keep = to_sbuf(nc.scalar.copy, acc_late, late, "w_raw1")
+        acc_late = product(first_codes[:], w_scales[:, 0:P], "acc_late")
         scatter(windows[0], keep_list, keep_weight, u_early, early)
-        scatter(windows[0], gone_list, gone_weight, u_early, early)
-        second_codes = pool.tile([P, P], U32, name="u_early", align_bytes=64)
+        second_codes = pool.tile([P, P], U32, name="second_codes", align_bytes=64)
         quantize(E4M3, second_codes[:], w_scales[:, P : 2 * P], w_second)
-        high_codes = pool.tile([P, 2 * P], U32, name="high_codes", align_bytes=64)
-        quantize(E4M3, high_codes[:], w_scales[:, 2 * P :], w_high)
-        last = pool.tile([P, TOKENS], F32, name="w_high", align_bytes=64)
+        scatter(windows[0], gone_list, gone_weight, u_early, early)
+        quantize_high_lanes(1)
+        acc1 = product(second_codes[:], w_scales[:, P : 2 * P], "acc1")
+        u1 = pool.tile([P, MERGED], F32, name="u1", align_bytes=64)
+        nc.scalar.copy(out=u1[:, early], in_=acc1[:, early])
+        u_late = to_sbuf(nc.scalar.copy, acc_late, late, "second_codes")
+        nc.scalar.copy(out=u1[:, late], in_=acc1[:, late])
+        scatter(windows[1], keep_list, keep_weight, u1[:, early], early)
+        scatter(windows[0], keep_list, keep_weight, u_late, late)
+        scatter(windows[1], keep_list, keep_weight, u1[:, late], late)
+        scatter(windows[0], gone_list, gone_weight, u_late, late)
+        scatter(windows[1], gone_list, gone_weight, u1[:], whole)
+        u2 = to_sbuf(nc.scalar.copy, product(high_codes[:, 0:P], w_scales[:, 2 * P : 3 * P], "acc2"), whole, "u2")
+        u3 = to_sbuf(nc.scalar.copy, product(high_codes[:, P:], w_scales[:, 3 * P :], "acc0"), whole, "u3")
+        last = pool.tile([P, TOKENS], F32, name="w_high1", align_bytes=64)
         nc.gpsimd.memset(last[:, 0 : 3 * CHUNK].bitcast(I32), 0)
-        scatter(windows[0], keep_list, keep_weight, late_keep, late)
-        windows.append(pool.tile([P, TOKENS], F32, name="w_raw1", align_bytes=64))
+        windows.append(pool.tile([P, TOKENS], F32, name="high_codes", align_bytes=64))
         nc.gpsimd.memset(windows[2][:].bitcast(I32), 0)
         nc.gpsimd.memset(last[:, 3 * CHUNK :].bitcast(I32), 0)
-        u1 = to_sbuf(nc.scalar.copy, product(second_codes[:], w_scales[:, P : 2 * P]), whole, "u1")
-        late_gone = to_sbuf(nc.scalar.copy, acc_late, late, "u_early")
-        scatter(windows[1], keep_list, keep_weight, u1, whole)
-        scatter(windows[0], gone_list, gone_weight, late_gone, late)
-        scatter(windows[1], gone_list, gone_weight, u1, whole)
-        u2 = to_sbuf(nc.scalar.copy, product(high_codes[:, 0:P], w_scales[:, 2 * P : 3 * P]), whole, "u_early")
-        u3 = to_sbuf(nc.scalar.copy, product(high_codes[:, P:], w_scales[:, 3 * P :]), whole, "u3")
 
         out_rows = out_0.rearrange("(w t) c -> w t c", t=LANES)
         grouped_out = pool.tile([P, TOKENS * LANES], BF16, name="grouped_out", align_bytes=64)

@@ -48,8 +48,9 @@ def tile_attend_gmerge_pl_kernel(tc, W, dz, wk, wg, koffs, goffs, out_0, out_1, 
         nc.sync.dma_start(out=w_raw[0][:], in_=w_rows[:, :, 0:HALF])
         nc.sync.dma_start(keep_list[:], koffs)
         nc.sync.dma_start(out=dz_raw[1][:], in_=dz_rows[:, :, HALF:MERGED])
-        nc.sync.dma_start(out=keep_weight[:], in_=wk)
+        nc.sync.dma_start(out=keep_weight[:, 0:HALF], in_=wk[:, 0:HALF])
         nc.sync.dma_start(out=w_raw[1][:], in_=w_rows[:, :, HALF:FEATURES])
+        nc.sync.dma_start(out=keep_weight[:, HALF:], in_=wk[:, HALF:])
         nc.sync.dma_start(gone_list[:], goffs)
 
         early, late, whole = slice(0, HALF), slice(HALF, MERGED), slice(0, MERGED)
@@ -144,8 +145,8 @@ def tile_attend_gmerge_pl_kernel(tc, W, dz, wk, wg, koffs, goffs, out_0, out_1, 
         scatter(windows[0], keep_list, keep_weight, u_early, early)
         second_codes = pool.tile([P, P], U32, name="second_codes", align_bytes=64)
         quantize(E4M3, second_codes[:], w_scales[:, P : 2 * P], w_second)
-        scatter(windows[0], gone_list, gone_weight, u_early, early)
         quantize_high_lanes(1)
+        scatter(windows[0], gone_list, gone_weight, u_early, early)
         acc1 = product(second_codes[:], w_scales[:, P : 2 * P], "acc1")
         u1 = pool.tile([P, MERGED], F32, name="u1", align_bytes=64)
         nc.scalar.copy(out=u1[:, early], in_=acc1[:, early])
@@ -208,8 +209,8 @@ def tile_attend_gmerge_pl_kernel(tc, W, dz, wk, wg, koffs, goffs, out_0, out_1, 
         scatter(last, keep_list, keep_weight, u3[:, early], early)
         scatter(windows[2], gone_list, gone_weight, u2, whole)
         nc.sync.dma_start(out=out_rows[:, 2, :], in_=windows[2][:])
-        for c in (0, 2, 1, 3):
-            round_into_lanes(nc.scalar.copy, windows[2], 2, c * CHUNK + FILL * (c >= FILL_CHUNK), (c + 1) * CHUNK)
+        for first, stop in ((0, 512), (1024 + FILL, 1536), (512, 1024), (1536 + FILL, 1792), (1808, 2048)):
+            round_into_lanes(nc.scalar.copy, windows[2], 2, first, stop)
         scatter(last, keep_list, keep_weight, u3[:, late], late)
         round_into_lanes(nc.vector.tensor_copy, windows[2], 2, FILL_CHUNK * CHUNK, FILL_CHUNK * CHUNK + FILL)
         scatter(last, gone_list, gone_weight, u3, whole)
@@ -217,32 +218,35 @@ def tile_attend_gmerge_pl_kernel(tc, W, dz, wk, wg, koffs, goffs, out_0, out_1, 
 
         out_words = out_1.rearrange("a p c t -> (a p) (c t)").bitcast(I32)
         out_scales = pool.tile([P, 2 * CHUNK], U8, name="out_scales", align_bytes=64)
-        out_codes = [pool.tile([P, CHUNK], U32, name=f"out_codes{c}", align_bytes=64) for c in range(CHUNKS)]
+        stores = ((0, 512), (512, 1024), (1024, 1536), (1536, 1792), (1792, 2048))
+        out_codes = {first: pool.tile([P, stop - first], U32, name=f"out_codes{first}", align_bytes=64) for first, stop in stores}
 
         def quantize_tokens(first, stop):
-            c, at = divmod(first, CHUNK)
-            column = (c % 2) * CHUNK + at
+            depth, column = divmod(first, 2 * CHUNK)
+            store = max(start for start in out_codes if start <= first)
             nc.vector.quantize_mx(
-                out=out_codes[c][:, at : at + stop - first].bitcast(E4M3),
-                scales=out_scales[4 * (c // 2) : P, column : column + stop - first],
+                out=out_codes[store][:, first - store : stop - store].bitcast(E4M3),
+                scales=out_scales[4 * depth : P, column : column + stop - first],
                 in_=grouped_out[:, first * LANES : stop * LANES],
             )
 
-        def store_chunk(c):
-            nc.sync.dma_start(out=out_words[:, c * CHUNK : (c + 1) * CHUNK], in_=out_codes[c][:].bitcast(I32))
+        def store_words(first, stop):
+            nc.sync.dma_start(out=out_words[:, first:stop], in_=out_codes[first][:].bitcast(I32))
 
-        round_into_lanes(nc.vector.tensor_copy, windows[2], 2, 3 * CHUNK, 3 * CHUNK + FILL)
+        round_into_lanes(nc.vector.tensor_copy, windows[2], 2, 1536, 1536 + FILL)
         round_into_lanes(nc.vector.tensor_copy, last, 3, 0, VECTOR_FIRST)
-        round_into_lanes(nc.vector.tensor_copy, last, 3, VECTOR_FIRST, VECTOR_TOKENS)
-        round_into_lanes(nc.scalar.copy, last, 3, VECTOR_TOKENS, 3 * CHUNK)
-        round_into_lanes(nc.scalar.copy, last, 3, 3 * CHUNK, 3 * CHUNK + HALF)
-        round_into_lanes(nc.scalar.copy, last, 3, 3 * CHUNK + HALF, TOKENS)
-        for c in range(CHUNKS - 1):
-            quantize_tokens(c * CHUNK, (c + 1) * CHUNK)
-            store_chunk(c)
-        quantize_tokens(3 * CHUNK, 3 * CHUNK + HALF)
-        quantize_tokens(3 * CHUNK + HALF, TOKENS)
-        store_chunk(3)
+        round_into_lanes(nc.vector.tensor_copy, last, 3, VECTOR_FIRST, 1024)
+        round_into_lanes(nc.scalar.copy, last, 3, 1024, 1536)
+        round_into_lanes(nc.scalar.copy, windows[2], 2, 1792, 1808)
+        round_into_lanes(nc.scalar.copy, last, 3, 1536, 1792)
+        round_into_lanes(nc.scalar.copy, last, 3, 1920, 2048)
+        for first, stop in stores[:3]:
+            quantize_tokens(first, stop)
+            store_words(first, stop)
+        round_into_lanes(nc.vector.tensor_copy, last, 3, 1792, 1920)
+        for first, stop in stores[3:]:
+            quantize_tokens(first, stop)
+            store_words(first, stop)
         scale_rows = out_2.rearrange("a b c -> (a b) c").bitcast(I32).rearrange("b (c w) -> c b w", c=2)
         for q in range(4):
             queue = nc.sync if q % 2 == 0 else nc.scalar

@@ -1,7 +1,6 @@
 from contextlib import ExitStack
 
 import concourse.mybir as mybir
-from concourse.masks import make_identity
 
 F32 = mybir.dt.float32
 BF16 = mybir.dt.bfloat16
@@ -12,6 +11,7 @@ U8 = mybir.dt.uint8
 E4M3 = mybir.dt.float8_e4m3fn_x4
 E5M2 = mybir.dt.float8_e5m2_x4
 MULT = mybir.AluOpType.mult
+COPY = mybir.ActivationFunctionType.Copy
 
 P = 128
 LANES = 4
@@ -19,14 +19,8 @@ MERGED = 512
 FEATURES = 512
 TOKENS = 2048
 HALF = 256
-GROUPS = FEATURES // P
-CHUNK = 512
-CHUNKS = TOKENS // CHUNK
-BLOCKS = CHUNK // P
-VECTOR_FIRST = 640
-VECTOR_TOKENS = 1152
-FILL = 192
-FILL_CHUNK = 2
+PAIR_CUTS = (0, 256, 1024, 2048)
+PLANE = 1024
 
 FLOPS = 2 * 512 * 512 * 512
 
@@ -37,216 +31,172 @@ def tile_attend_gmerge_pl_kernel(tc, W, dz, wk, wg, koffs, goffs, out_0, out_1, 
         pool = ctx.enter_context(tc.tile_pool(name="held", bufs=1))
         psum = ctx.enter_context(tc.psum_pool(name="psum", bufs=1))
 
+        early, late, whole = slice(0, HALF), slice(HALF, MERGED), slice(0, MERGED)
         keep_list = pool.tile([P, MERGED // 16], U16, name="keep_list")
         gone_list = pool.tile([P, MERGED // 16], U16, name="gone_list")
         keep_weight = pool.tile([P, MERGED], F32, name="keep_weight")
+        gone_weight = pool.tile([P, MERGED], F32, name="gone_weight")
         dz_rows = dz.rearrange("(p j) i -> p j i", j=LANES)
         w_rows = W.rearrange("(p j) d -> p j d", j=LANES)
         dz_raw = [pool.tile([P, LANES, HALF], F32, name=f"dz_raw{h}") for h in range(2)]
-        w_raw = [pool.tile([P, LANES, HALF], F32, name=f"w_raw{h}", align_bytes=64) for h in range(2)]
-        nc.sync.dma_start(out=dz_raw[0][:], in_=dz_rows[:, :, 0:HALF])
-        nc.sync.dma_start(out=w_raw[0][:], in_=w_rows[:, :, 0:HALF])
+        w_raw = [pool.tile([P, 2, FEATURES], F32, name=f"w_raw{a}") for a in range(2)]
+        nc.sync.dma_start(out=dz_raw[0][:], in_=dz_rows[:, :, early])
+        nc.sync.dma_start(out=w_raw[0][:], in_=w_rows[:, 0:2, :])
+        nc.sync.dma_start(out=w_raw[1][:], in_=w_rows[:, 2:4, :])
         nc.sync.dma_start(keep_list[:], koffs)
-        nc.sync.dma_start(out=dz_raw[1][:], in_=dz_rows[:, :, HALF:MERGED])
-        nc.sync.dma_start(out=keep_weight[:, 0:HALF], in_=wk[:, 0:HALF])
-        nc.sync.dma_start(out=w_raw[1][:], in_=w_rows[:, :, HALF:FEATURES])
-        nc.sync.dma_start(out=keep_weight[:, HALF:], in_=wk[:, HALF:])
+        nc.sync.dma_start(out=keep_weight[:, early], in_=wk[:, early])
+        nc.sync.dma_start(out=dz_raw[1][:], in_=dz_rows[:, :, late])
         nc.sync.dma_start(gone_list[:], goffs)
+        nc.sync.dma_start(out=gone_weight[:], in_=wg)
+        nc.sync.dma_start(out=keep_weight[:, late], in_=wk[:, late])
+        keep, gone = (keep_list, keep_weight), (gone_list, gone_weight)
 
-        early, late, whole = slice(0, HALF), slice(HALF, MERGED), slice(0, MERGED)
+        windows = [pool.tile([P, TOKENS], F32, name=f"window{t}") for t in range(3)]
+        nc.gpsimd.memset(windows[0][:].bitcast(I32), 0)
+        nc.gpsimd.memset(windows[1][:].bitcast(I32), 0)
+        nc.vector.memset(windows[2][:, 0 : PLANE - 1].bitcast(I32), 0)
+        nc.vector.memset(windows[2][:, PLANE - 1 :].bitcast(I32), 0)
+
         dz_codes = pool.tile([P, MERGED], U32, name="dz_codes", align_bytes=64)
         dz_scales = pool.tile([P, MERGED], U8, name="dz_scales", align_bytes=64)
-        nc.vector.memset(dz_codes[:, HALF - 1 :], 0)
-        nc.vector.memset(dz_scales[:, HALF - 4 :].bitcast(U32), 0)
-        windows = [pool.tile([P, TOKENS], F32, name=f"window{g}") for g in range(2)]
-        nc.vector.memset(windows[0][:, 0 : 2 * CHUNK - 1].bitcast(I32), 0)
-        nc.vector.memset(windows[0][:, 2 * CHUNK - 1 :].bitcast(I32), 0)
-        identity = pool.tile([P, P], F32, name="identity")
-        make_identity(nc, identity[:])
-        nc.gpsimd.memset(windows[1][:].bitcast(I32), 0)
+        w_codes = pool.tile([P, FEATURES], U32, name="w_codes", align_bytes=64)
+        w_scales = pool.tile([P, FEATURES], U8, name="w_scales", align_bytes=64)
+        w_grouped = [pool.tile([P, 2, P, LANES], BF16, name=f"w_grouped{u}", align_bytes=64) for u in range(2)]
 
-        def round_and_group(shares, raw, name):
-            grouped = pool.tile([P, raw.shape[2] * LANES], BF16, name=name, align_bytes=64)
-            for copy, quads in shares:
-                copy(
-                    out=grouped[:].rearrange("p (c i j) -> p c j i", i=4, j=LANES)[:, quads],
-                    in_=raw.rearrange("p j (c i) -> p c j i", i=4)[:, quads],
-                )
-            return grouped[:]
+        def group_dz(copy, h):
+            grouped = pool.tile([P, HALF * LANES], BF16, name=f"dz_grouped{h}", align_bytes=64)
+            copy(
+                out=grouped[:].rearrange("p (c i j) -> p c j i", i=4, j=LANES),
+                in_=dz_raw[h][:].rearrange("p j (c i) -> p c j i", i=4),
+            )
+            return grouped
 
-        def group_low_lanes(shares, h):
-            grouped = pool.tile([P, P * LANES], BF16, name=f"w_low{h}", align_bytes=64)
-            for copy, words in shares:
-                copy(
-                    out=grouped[:].rearrange("p (w e j) -> p w j e", e=2, j=LANES)[:, words],
-                    in_=w_raw[h][:].rearrange("p j (w t) -> p w j t", t=LANES)[:, words, :, 0:2],
-                )
-            return grouped[:]
-
-        w_high = [pool.tile([P, P * LANES], BF16, name=f"w_high{h}", align_bytes=64) for h in range(2)]
-
-        def group_high_lanes(h):
-            nc.scalar.copy(
-                out=w_high[h][:].rearrange("p (e w j) -> p w j e", e=2, j=LANES),
-                in_=w_raw[h][:].rearrange("p j (w t) -> p w j t", t=LANES)[:, :, :, 2:4],
+        def group_w(copy, u, a):
+            copy(
+                out=w_grouped[u][:, :, :, 2 * a : 2 * a + 2].rearrange("p e w j -> p w j e"),
+                in_=w_raw[a][:].rearrange("p j (w t) -> p w j t", t=LANES)[:, :, :, 2 * u : 2 * u + 2],
             )
 
-        def quantize(dtype, codes, scales, grouped):
-            nc.vector.quantize_mx(out=codes.bitcast(dtype), scales=scales, in_=grouped)
+        def quantize_dz(columns, grouped):
+            nc.vector.quantize_mx(out=dz_codes[:, columns].bitcast(E5M2), scales=dz_scales[:, columns], in_=grouped[:])
 
-        def product(codes, scales, bank):
-            acc = psum.tile([P, MERGED], F32, name=bank)
+        def quantize_w(first, stop):
+            u, columns = first // 2, slice(first * P, stop * P)
+            nc.vector.quantize_mx(
+                out=w_codes[:, columns].bitcast(E4M3),
+                scales=w_scales[:, columns],
+                in_=w_grouped[u][:, first - 2 * u : stop - 2 * u].rearrange("p e w j -> p (e w j)"),
+            )
+
+        def product(t, columns, bank):
+            acc = psum.tile([P, columns.stop - columns.start], F32, name=bank)
             nc.tensor.matmul_mx(
                 out=acc[:],
-                lhsT=codes.bitcast(E4M3),
-                lhsT_scale=scales,
-                rhs=dz_codes[:].bitcast(E5M2),
-                rhs_scale=dz_scales[:],
+                lhsT=w_codes[:, t * P : (t + 1) * P].bitcast(E4M3),
+                lhsT_scale=w_scales[:, t * P : (t + 1) * P],
+                rhs=dz_codes[:, columns].bitcast(E5M2),
+                rhs_scale=dz_scales[:, columns],
                 start=True,
                 stop=True,
             )
             return acc
 
-        def to_sbuf(copy, acc, columns, name):
-            u = pool.tile([P, columns.stop - columns.start], F32, name=name, align_bytes=64)
-            copy(out=u[:], in_=acc[:, columns])
-            return u[:]
+        def weigh(acc, side, columns, name):
+            weighed = pool.tile([P, columns.stop - columns.start], F32, name=name)
+            nc.vector.tensor_tensor(weighed[:], acc, side[1][:, columns], MULT)
+            return weighed
 
-        def scatter(window, offsets, weight, u, columns):
-            entries = slice(columns.start // 16, columns.stop // 16)
-            nc.vector.tensor_tensor(window[:].indirect(offsets[:, entries]), u, weight[:, columns], MULT)
+        def to_sbuf(acc, name):
+            u = pool.tile([P, acc.shape[1]], F32, name=name)
+            nc.vector.tensor_copy(out=u[:], in_=acc)
+            return u
 
-        w_scales = pool.tile([P, FEATURES], U8, name="w_scales", align_bytes=64)
-        first_codes = pool.tile([P, P], U32, name="first_codes", align_bytes=64)
+        def places(window, side, columns):
+            return window[:].indirect(side[0][:, columns.start // 16 : columns.stop // 16])
 
-        high_codes = pool.tile([P, 2 * P], U32, name="high_codes", align_bytes=64)
+        def scalar_scatter(window, side, columns, weighed):
+            nc.scalar.activation(places(window, side, columns), weighed, COPY)
 
-        def quantize_high_lanes(h):
-            for e in range(2):
-                first = e * P + h * 64
-                quantize(E4M3, high_codes[:, first : first + 64], w_scales[:, 2 * P + first : 2 * P + first + 64], w_high[h][:, e * HALF : (e + 1) * HALF])
+        def vector_scatter(window, side, columns, u):
+            nc.vector.tensor_tensor(places(window, side, columns), u, side[1][:, columns], MULT)
 
-        for n, copy in enumerate((nc.vector.tensor_copy, nc.scalar.copy)):
-            columns = slice(n * P, (n + 1) * P)
-            grouped = round_and_group(((copy, slice(0, 32)),), dz_raw[0][:, :, columns], f"dz_early{n}")
-            quantize(E5M2, dz_codes[:, columns], dz_scales[:, columns], grouped)
-        quantize(E4M3, first_codes[:], w_scales[:, 0:P], group_low_lanes(((nc.vector.tensor_copy, slice(0, 40)), (nc.scalar.copy, slice(40, 64))), 0))
-        acc = product(first_codes[:], w_scales[:, 0:P], "acc0")
-        u_early = to_sbuf(nc.vector.tensor_copy, acc, early, "u_early")
-        group_high_lanes(0)
-        dz_late = round_and_group(((nc.vector.tensor_copy, slice(0, 40)), (nc.scalar.copy, slice(40, 64))), dz_raw[1][:], "dz_late")
-        gone_weight = pool.tile([P, MERGED], F32, name="dz_raw1")
-        nc.sync.dma_start(out=gone_weight[:], in_=wg)
-        quantize_high_lanes(0)
-        quantize(E5M2, dz_codes[:, late], dz_scales[:, late], dz_late)
-        w_second = group_low_lanes(((nc.scalar.copy, slice(0, 64)),), 1)
-        group_high_lanes(1)
-        acc_late = product(first_codes[:], w_scales[:, 0:P], "acc_late")
-        scatter(windows[0], keep_list, keep_weight, u_early, early)
-        second_codes = pool.tile([P, P], U32, name="second_codes", align_bytes=64)
-        quantize(E4M3, second_codes[:], w_scales[:, P : 2 * P], w_second)
-        quantize_high_lanes(1)
-        scatter(windows[0], gone_list, gone_weight, u_early, early)
-        acc1 = product(second_codes[:], w_scales[:, P : 2 * P], "acc1")
-        u1 = pool.tile([P, MERGED], F32, name="u1", align_bytes=64)
-        nc.scalar.copy(out=u1[:, early], in_=acc1[:, early])
-        u_late = to_sbuf(nc.scalar.copy, acc_late, late, "second_codes")
-        nc.scalar.copy(out=u1[:, late], in_=acc1[:, late])
-        scatter(windows[1], keep_list, keep_weight, u1[:, early], early)
-        scatter(windows[0], keep_list, keep_weight, u_late, late)
-        scatter(windows[1], keep_list, keep_weight, u1[:, late], late)
-        scatter(windows[0], gone_list, gone_weight, u_late, late)
-        scatter(windows[1], gone_list, gone_weight, u1[:], whole)
-        u2 = to_sbuf(nc.scalar.copy, product(high_codes[:, 0:P], w_scales[:, 2 * P : 3 * P], "acc2"), whole, "u2")
-        u3 = to_sbuf(nc.scalar.copy, product(high_codes[:, P:], w_scales[:, 3 * P :], "acc0"), whole, "u3")
-        last = pool.tile([P, TOKENS], F32, name="w_high1", align_bytes=64)
-        nc.gpsimd.memset(last[:, 0 : 3 * CHUNK].bitcast(I32), 0)
-        windows.append(pool.tile([P, TOKENS], F32, name="high_codes", align_bytes=64))
-        nc.gpsimd.memset(windows[2][:].bitcast(I32), 0)
-        nc.gpsimd.memset(last[:, 3 * CHUNK :].bitcast(I32), 0)
+        quantize_dz(early, group_dz(nc.scalar.copy, 0))
+        for a in range(2):
+            group_w(nc.vector.tensor_copy, 0, a)
+            group_w(nc.scalar.copy, 1, a)
+        quantize_w(0, 1)
+        quantize_w(1, 2)
+        acc = product(0, early, "acc0_early")
+        scalar_scatter(windows[0], keep, early, weigh(acc[:], keep, early, "keep0_early")[:])
+        dz_late = group_dz(nc.vector.tensor_copy, 1)
+        scalar_scatter(windows[0], gone, early, weigh(acc[:], gone, early, "gone0_early")[:])
+        quantize_dz(late, dz_late)
+        quantize_w(2, 4)
+        windows.append(pool.tile([P, TOKENS], F32, name="dz_grouped1", align_bytes=64))
+        nc.gpsimd.memset(windows[3][:].bitcast(I32), 0)
+
+        acc = product(0, late, "acc0_late")
+        accs = {t: product(t, whole, f"acc{t}") for t in (2, 1, 3)}
+        scalar_scatter(windows[0], keep, late, weigh(acc[:], keep, late, "keep0_late")[:])
+        scalar_scatter(windows[0], gone, late, weigh(acc[:], gone, late, "gone0_late")[:])
+        u2_late = to_sbuf(accs[2][:, late], "u2_late")
+        keep2 = weigh(accs[2][:], keep, whole, "keep2")
+        gone2 = weigh(accs[2][:, early], gone, early, "gone2")
+        vector_scatter(windows[2], gone, late, u2_late[:])
+        scalar_scatter(windows[2], keep, early, keep2[:, early])
+        scalar_scatter(windows[2], keep, late, keep2[:, late])
+        scalar_scatter(windows[2], gone, early, gone2[:])
+        u1 = to_sbuf(accs[1][:], "u1")
+        for side, name in ((keep, "keep3"), (gone, "gone3")):
+            weighed = weigh(accs[3][:], side, whole, name)
+            for columns in (early, late):
+                scalar_scatter(windows[3], side, columns, weighed[:, columns])
 
         out_rows = out_0.rearrange("(w t) c -> w t c", t=LANES)
-        grouped_out = pool.tile([P, TOKENS * LANES], BF16, name="grouped_out", align_bytes=64)
-        chunk_values = [grouped_out[:, c * CHUNK * LANES : (c + 1) * CHUNK * LANES] for c in range(CHUNKS)]
-        pairs = [pool.tile([P, BLOCKS, 2, P], BF16, name=f"pairs{c}") for c in range(CHUNKS)]
+        cuts = list(zip(PAIR_CUTS, PAIR_CUTS[1:]))
+        pairs = {first: pool.tile([P, 2, stop - first, 2], BF16, name=f"pairs{first}") for first, stop in cuts}
 
-        def turn(window, h, c):
-            turned = psum.tile([P, BLOCKS, P], F32, name=f"bank{c}")
-            for b in range(BLOCKS):
-                first = c * CHUNK + b * P
-                nc.tensor.transpose(turned[:, b, :], window[:, first : first + P], identity[:])
-            nc.scalar.copy(out=pairs[c][:, :, h, :], in_=turned[:])
+        def finish(t):
+            nc.sync.dma_start(out=out_rows[:, t, :], in_=windows[t][:])
+            for first, stop in cuts:
+                nc.vector.tensor_copy(out=pairs[first][:, t // 2, :, t % 2], in_=windows[t][:, first:stop])
 
-        def turn_back(c):
-            back = psum.tile([P, CHUNK], F32, name=f"bank{c}")
-            words = pairs[c][:].rearrange("p b h q -> p (b h q)").bitcast(F32)
-            for b in range(BLOCKS):
-                nc.tensor.transpose(back[:, b * P : (b + 1) * P], words[:, b * P : (b + 1) * P], identity[:])
-            first = FILL * (c == FILL_CHUNK)
-            if first:
-                nc.scalar.copy(
-                    out=chunk_values[c].rearrange("p (c t) -> p c t", t=LANES)[:, 0:first, 0:2],
-                    in_=back[:, 0:first].bitcast(BF16).rearrange("p (c t) -> p c t", t=2),
-                )
-            nc.scalar.copy(
-                out=chunk_values[c].bitcast(F32).rearrange("p (c u) -> p c u", u=2)[:, first:],
-                in_=back[:, first:].unsqueeze(2).to_broadcast([P, CHUNK - first, 2]),
-            )
-
-        def round_into_lanes(copy, window, t, first, stop):
-            copy(
-                out=grouped_out[:].rearrange("p (c t) -> p c t", t=LANES)[:, first:stop, t:LANES],
-                in_=window[:, first:stop].unsqueeze(2).to_broadcast([P, stop - first, LANES - t]),
-            )
-
-        for g in range(2):
-            nc.sync.dma_start(out=out_rows[g * 64 : (g + 1) * 64, 0:2, :], in_=windows[g][:])
-            for c in range(CHUNKS):
-                turn(windows[g], g, c)
-        for c in range(CHUNKS):
-            turn_back(c)
-        scatter(windows[2], keep_list, keep_weight, u2, whole)
-        scatter(last, keep_list, keep_weight, u3[:, early], early)
-        scatter(windows[2], gone_list, gone_weight, u2, whole)
-        nc.sync.dma_start(out=out_rows[:, 2, :], in_=windows[2][:])
-        for first, stop in ((0, 512), (1024 + FILL, 1536), (512, 1024), (1536 + FILL, 1792), (1808, 2048)):
-            round_into_lanes(nc.scalar.copy, windows[2], 2, first, stop)
-        scatter(last, keep_list, keep_weight, u3[:, late], late)
-        round_into_lanes(nc.vector.tensor_copy, windows[2], 2, FILL_CHUNK * CHUNK, FILL_CHUNK * CHUNK + FILL)
-        scatter(last, gone_list, gone_weight, u3, whole)
-        nc.sync.dma_start(out=out_rows[:, 3, :], in_=last[:])
+        vector_scatter(windows[1], keep, whole, u1[:])
+        finish(0)
+        vector_scatter(windows[1], gone, whole, u1[:])
+        finish(2)
+        finish(1)
+        finish(3)
 
         out_words = out_1.rearrange("a p c t -> (a p) (c t)").bitcast(I32)
-        out_scales = pool.tile([P, 2 * CHUNK], U8, name="out_scales", align_bytes=64)
+        out_scales = pool.tile([P, PLANE], U8, name="out_scales", align_bytes=64)
         stores = ((0, 512), (512, 1024), (1024, 1536), (1536, 1792), (1792, 2048))
-        out_codes = {first: pool.tile([P, stop - first], U32, name=f"out_codes{first}", align_bytes=64) for first, stop in stores}
+        grouped_out = {first: pool.tile([P, (stop - first) * LANES], BF16, name=f"grouped_out{first}", align_bytes=64) for first, stop in stores}
 
-        def quantize_tokens(first, stop):
-            depth, column = divmod(first, 2 * CHUNK)
-            store = max(start for start in out_codes if start <= first)
-            nc.vector.quantize_mx(
-                out=out_codes[store][:, first - store : stop - store].bitcast(E4M3),
-                scales=out_scales[4 * depth : P, column : column + stop - first],
-                in_=grouped_out[:, first * LANES : stop * LANES],
+        def weave(copy, dtype, first, stop):
+            cut = max(c for c in pairs if c <= first)
+            store = max(c for c in grouped_out if c <= first)
+            words = pairs[cut][:].rearrange("p u c e -> p (u c e)").bitcast(dtype).rearrange("p (u c) -> p c u", u=2)
+            copy(
+                out=grouped_out[store][:].bitcast(dtype).rearrange("p (c u) -> p c u", u=2)[:, first - store : stop - store],
+                in_=words[:, first - cut : stop - cut],
             )
 
-        def store_words(first, stop):
-            nc.sync.dma_start(out=out_words[:, first:stop], in_=out_codes[first][:].bitcast(I32))
+        def quantize_tokens(first, stop):
+            depth, column = divmod(first, PLANE)
+            codes = pool.tile([P, stop - first], U32, name=f"out_codes{first}", align_bytes=64)
+            nc.vector.quantize_mx(
+                out=codes[:].bitcast(E4M3),
+                scales=out_scales[4 * depth : P, column : column + stop - first],
+                in_=grouped_out[first][:],
+            )
+            nc.sync.dma_start(out=out_words[:, first:stop], in_=codes[:].bitcast(I32))
 
-        round_into_lanes(nc.vector.tensor_copy, windows[2], 2, 1536, 1536 + FILL)
-        round_into_lanes(nc.vector.tensor_copy, last, 3, 0, VECTOR_FIRST)
-        round_into_lanes(nc.vector.tensor_copy, last, 3, VECTOR_FIRST, 1024)
-        round_into_lanes(nc.scalar.copy, last, 3, 1024, 1536)
-        round_into_lanes(nc.scalar.copy, windows[2], 2, 1792, 1808)
-        round_into_lanes(nc.scalar.copy, last, 3, 1536, 1792)
-        round_into_lanes(nc.scalar.copy, last, 3, 1920, 2048)
-        for first, stop in stores[:3]:
-            quantize_tokens(first, stop)
-            store_words(first, stop)
-        round_into_lanes(nc.vector.tensor_copy, last, 3, 1792, 1920)
-        for first, stop in stores[3:]:
-            quantize_tokens(first, stop)
-            store_words(first, stop)
+        for first, stop in ((0, 256), (256, 512), (512, 1024), (1024, 1536), (1536, 1792)):
+            weave(nc.scalar.copy, U32, first, stop)
+        weave(nc.vector.tensor_copy, I32, 1792, 2048)
+        for s in (0, 1, 4, 2, 3):
+            quantize_tokens(*stores[s])
         scale_rows = out_2.rearrange("a b c -> (a b) c").bitcast(I32).rearrange("b (c w) -> c b w", c=2)
         for q in range(4):
             queue = nc.sync if q % 2 == 0 else nc.scalar

@@ -21,6 +21,7 @@ TOKENS = 2048
 HALF = 256
 PAIR_CUTS = (0, 256, 1024, 2048)
 PLANE = 1024
+VECTOR_ZEROES = 768
 
 FLOPS = 2 * 512 * 512 * 512
 
@@ -44,18 +45,19 @@ def tile_attend_gmerge_pl_kernel(tc, W, dz, wk, wg, koffs, goffs, out_0, out_1, 
         nc.sync.dma_start(out=w_raw[0][:], in_=w_rows[:, 0:2, :])
         nc.sync.dma_start(out=w_raw[1][:], in_=w_rows[:, 2:4, :])
         nc.sync.dma_start(keep_list[:], koffs)
-        nc.sync.dma_start(out=keep_weight[:, early], in_=wk[:, early])
+        nc.sync.dma_start(out=keep_weight[:], in_=wk)
         nc.sync.dma_start(out=dz_raw[1][:], in_=dz_rows[:, :, late])
         nc.sync.dma_start(gone_list[:], goffs)
         nc.sync.dma_start(out=gone_weight[:], in_=wg)
-        nc.sync.dma_start(out=keep_weight[:, late], in_=wk[:, late])
-        keep, gone = (keep_list, keep_weight), (gone_list, gone_weight)
+        keep, gone = (keep_list, keep_weight, "keep"), (gone_list, gone_weight, "gone")
 
         windows = [pool.tile([P, TOKENS], F32, name=f"window{t}") for t in range(3)]
         nc.gpsimd.memset(windows[0][:].bitcast(I32), 0)
-        nc.gpsimd.memset(windows[1][:].bitcast(I32), 0)
         nc.vector.memset(windows[2][:, 0 : PLANE - 1].bitcast(I32), 0)
         nc.vector.memset(windows[2][:, PLANE - 1 :].bitcast(I32), 0)
+        nc.vector.memset(windows[1][:, 1:VECTOR_ZEROES].bitcast(I32), 0)
+        nc.vector.memset(windows[1][:, 0:1].bitcast(I32), 0)
+        nc.gpsimd.memset(windows[1][:, VECTOR_ZEROES:].bitcast(I32), 0)
 
         dz_codes = pool.tile([P, MERGED], U32, name="dz_codes", align_bytes=64)
         dz_scales = pool.tile([P, MERGED], U8, name="dz_scales", align_bytes=64)
@@ -126,31 +128,37 @@ def tile_attend_gmerge_pl_kernel(tc, W, dz, wk, wg, koffs, goffs, out_0, out_1, 
             group_w(nc.scalar.copy, 1, a)
         quantize_w(0, 1)
         quantize_w(1, 2)
-        acc = product(0, early, "acc0_early")
-        scalar_scatter(windows[0], keep, early, weigh(acc[:], keep, early, "keep0_early")[:])
-        dz_late = group_dz(nc.vector.tensor_copy, 1)
-        scalar_scatter(windows[0], gone, early, weigh(acc[:], gone, early, "gone0_early")[:])
-        quantize_dz(late, dz_late)
         quantize_w(2, 4)
+        accs = [product(t, early, f"acc{t}_early") for t in range(3)]
+
+        def by_scalar(t, side, columns):
+            scalar_scatter(windows[t], side, columns, weigh(accs[t][:], side, columns, f"{side[2]}{t}_{columns.start}")[:])
+
+        by_scalar(0, keep, early)
+        by_scalar(1, keep, early)
+        dz_late = group_dz(nc.vector.tensor_copy, 1)
+        u2 = pool.tile([P, MERGED], F32, name="u2")
+        nc.vector.tensor_copy(out=u2[:, early], in_=accs[2][:])
+        quantize_dz(late, dz_late)
         windows.append(pool.tile([P, TOKENS], F32, name="dz_grouped1", align_bytes=64))
         nc.gpsimd.memset(windows[3][:].bitcast(I32), 0)
-
-        acc = product(0, late, "acc0_late")
-        accs = {t: product(t, whole, f"acc{t}") for t in (2, 1, 3)}
-        scalar_scatter(windows[0], keep, late, weigh(acc[:], keep, late, "keep0_late")[:])
-        scalar_scatter(windows[0], gone, late, weigh(acc[:], gone, late, "gone0_late")[:])
-        u2_late = to_sbuf(accs[2][:, late], "u2_late")
-        keep2 = weigh(accs[2][:], keep, whole, "keep2")
-        gone2 = weigh(accs[2][:, early], gone, early, "gone2")
-        vector_scatter(windows[2], gone, late, u2_late[:])
-        scalar_scatter(windows[2], keep, early, keep2[:, early])
-        scalar_scatter(windows[2], keep, late, keep2[:, late])
-        scalar_scatter(windows[2], gone, early, gone2[:])
-        u1 = to_sbuf(accs[1][:], "u1")
-        for side, name in ((keep, "keep3"), (gone, "gone3")):
-            weighed = weigh(accs[3][:], side, whole, name)
-            for columns in (early, late):
-                scalar_scatter(windows[3], side, columns, weighed[:, columns])
+        by_scalar(0, gone, early)
+        by_scalar(1, gone, early)
+        vector_scatter(windows[2], gone, early, u2[:, early])
+        accs = [product(t, late, f"acc{t}_late") for t in range(3)]
+        acc3 = product(3, whole, "acc3")
+        by_scalar(0, keep, late)
+        by_scalar(1, keep, late)
+        nc.vector.tensor_copy(out=u2[:, late], in_=accs[2][:])
+        u3 = to_sbuf(acc3[:, early], "u3")
+        by_scalar(0, gone, late)
+        vector_scatter(windows[2], keep, whole, u2[:])
+        vector_scatter(windows[3], gone, early, u3[:])
+        scalar_scatter(windows[3], keep, early, weigh(acc3[:, early], keep, early, "keep3_early")[:])
+        vector_scatter(windows[2], gone, late, u2[:, late])
+        by_scalar(1, gone, late)
+        scalar_scatter(windows[3], keep, late, weigh(acc3[:, late], keep, late, "keep3_late")[:])
+        scalar_scatter(windows[3], gone, late, weigh(acc3[:, late], gone, late, "gone3")[:])
 
         out_rows = out_0.rearrange("(w t) c -> w t c", t=LANES)
         cuts = list(zip(PAIR_CUTS, PAIR_CUTS[1:]))
@@ -161,12 +169,8 @@ def tile_attend_gmerge_pl_kernel(tc, W, dz, wk, wg, koffs, goffs, out_0, out_1, 
             for first, stop in cuts:
                 nc.vector.tensor_copy(out=pairs[first][:, t // 2, :, t % 2], in_=windows[t][:, first:stop])
 
-        vector_scatter(windows[1], keep, whole, u1[:])
-        finish(0)
-        vector_scatter(windows[1], gone, whole, u1[:])
-        finish(2)
-        finish(1)
-        finish(3)
+        for t in (0, 2, 1, 3):
+            finish(t)
 
         out_words = out_1.rearrange("a p c t -> (a p) (c t)").bitcast(I32)
         out_scales = pool.tile([P, PLANE], U8, name="out_scales", align_bytes=64)
@@ -199,8 +203,7 @@ def tile_attend_gmerge_pl_kernel(tc, W, dz, wk, wg, koffs, goffs, out_0, out_1, 
             quantize_tokens(*stores[s])
         scale_rows = out_2.rearrange("a b c -> (a b) c").bitcast(I32).rearrange("b (c w) -> c b w", c=2)
         for q in range(4):
-            queue = nc.sync if q % 2 == 0 else nc.scalar
-            queue.dma_start(
+            nc.sync.dma_start(
                 out=scale_rows[:, 4 * q : 4 * q + 4, :],
                 in_=out_scales[32 * q : 32 * q + 8, :].bitcast(I32),
             )

@@ -11,6 +11,7 @@ U8 = mybir.dt.uint8
 E4M3 = mybir.dt.float8_e4m3fn_x4
 E5M2 = mybir.dt.float8_e5m2_x4
 MULT = mybir.AluOpType.mult
+ADD = mybir.AluOpType.add
 COPY = mybir.ActivationFunctionType.Copy
 
 P = 128
@@ -19,8 +20,10 @@ MERGED = 512
 FEATURES = 512
 TOKENS = 2048
 HALF = 256
-PAIR_CUTS = (0, 256, 1024, 2048)
+PAIR_CUTS = (0, 128, 512, 1024, 2048)
 PLANE = 1024
+VECTOR_WORDS = 88
+LAST_SCATTER = 384
 VECTOR_ZEROES = 768
 
 FLOPS = 2 * 512 * 512 * 512
@@ -59,6 +62,9 @@ def tile_attend_gmerge_pl_kernel(tc, W, dz, wk, wg, koffs, goffs, out_0, out_1, 
         nc.vector.memset(windows[1][:, 0:1].bitcast(I32), 0)
         nc.gpsimd.memset(windows[1][:, VECTOR_ZEROES:].bitcast(I32), 0)
 
+        zeros = pool.tile([P, MERGED - LAST_SCATTER], F32, name="zeros")
+        nc.vector.memset(zeros[:], 0.0)
+
         dz_codes = pool.tile([P, MERGED], U32, name="dz_codes", align_bytes=64)
         dz_scales = pool.tile([P, MERGED], U8, name="dz_scales", align_bytes=64)
         w_codes = pool.tile([P, FEATURES], U32, name="w_codes", align_bytes=64)
@@ -73,10 +79,10 @@ def tile_attend_gmerge_pl_kernel(tc, W, dz, wk, wg, koffs, goffs, out_0, out_1, 
             )
             return grouped
 
-        def group_w(copy, u, a):
+        def group_w(copy, u, a, words=slice(0, P)):
             copy(
-                out=w_grouped[u][:, :, :, 2 * a : 2 * a + 2].rearrange("p e w j -> p w j e"),
-                in_=w_raw[a][:].rearrange("p j (w t) -> p w j t", t=LANES)[:, :, :, 2 * u : 2 * u + 2],
+                out=w_grouped[u][:, :, words, 2 * a : 2 * a + 2].rearrange("p e w j -> p w j e"),
+                in_=w_raw[a][:].rearrange("p j (w t) -> p w j t", t=LANES)[:, words, :, 2 * u : 2 * u + 2],
             )
 
         def quantize_dz(columns, grouped):
@@ -123,9 +129,11 @@ def tile_attend_gmerge_pl_kernel(tc, W, dz, wk, wg, koffs, goffs, out_0, out_1, 
             nc.vector.tensor_tensor(places(window, side, columns), u, side[1][:, columns], MULT)
 
         quantize_dz(early, group_dz(nc.scalar.copy, 0))
-        for a in range(2):
-            group_w(nc.vector.tensor_copy, 0, a)
-            group_w(nc.scalar.copy, 1, a)
+        group_w(nc.vector.tensor_copy, 0, 0)
+        group_w(nc.scalar.copy, 1, 0)
+        group_w(nc.vector.tensor_copy, 0, 1, slice(0, VECTOR_WORDS))
+        group_w(nc.scalar.copy, 0, 1, slice(VECTOR_WORDS, P))
+        group_w(nc.scalar.copy, 1, 1)
         quantize_w(0, 1)
         quantize_w(1, 2)
         quantize_w(2, 4)
@@ -134,10 +142,14 @@ def tile_attend_gmerge_pl_kernel(tc, W, dz, wk, wg, koffs, goffs, out_0, out_1, 
         def by_scalar(t, side, columns):
             scalar_scatter(windows[t], side, columns, weigh(accs[t][:], side, columns, f"{side[2]}{t}_{columns.start}")[:])
 
+        def rest_by_vector(side, weighed):
+            rest = slice(LAST_SCATTER, MERGED)
+            nc.vector.tensor_tensor(places(windows[3], side, rest), weighed[:, rest], zeros[:], ADD)
+
+        u2 = pool.tile([P, MERGED], F32, name="u2")
         by_scalar(0, keep, early)
         by_scalar(1, keep, early)
         dz_late = group_dz(nc.vector.tensor_copy, 1)
-        u2 = pool.tile([P, MERGED], F32, name="u2")
         nc.vector.tensor_copy(out=u2[:, early], in_=accs[2][:])
         quantize_dz(late, dz_late)
         windows.append(pool.tile([P, TOKENS], F32, name="dz_grouped1", align_bytes=64))
@@ -150,24 +162,28 @@ def tile_attend_gmerge_pl_kernel(tc, W, dz, wk, wg, koffs, goffs, out_0, out_1, 
         by_scalar(0, keep, late)
         by_scalar(1, keep, late)
         nc.vector.tensor_copy(out=u2[:, late], in_=accs[2][:])
-        u3 = to_sbuf(acc3[:, early], "u3")
+        gone3 = weigh(acc3[:], gone, whole, "gone3")
+        keep3 = weigh(acc3[:], keep, whole, "keep3")
         by_scalar(0, gone, late)
+        rest_by_vector(gone, gone3)
         vector_scatter(windows[2], keep, whole, u2[:])
-        vector_scatter(windows[3], gone, early, u3[:])
-        scalar_scatter(windows[3], keep, early, weigh(acc3[:, early], keep, early, "keep3_early")[:])
-        vector_scatter(windows[2], gone, late, u2[:, late])
+        rest_by_vector(keep, keep3)
+        scalar_scatter(windows[3], gone, slice(0, LAST_SCATTER), gone3[:, 0:LAST_SCATTER])
         by_scalar(1, gone, late)
-        scalar_scatter(windows[3], keep, late, weigh(acc3[:, late], keep, late, "keep3_late")[:])
-        scalar_scatter(windows[3], gone, late, weigh(acc3[:, late], gone, late, "gone3")[:])
+        vector_scatter(windows[2], gone, late, u2[:, late])
+        scalar_scatter(windows[3], keep, slice(0, LAST_SCATTER), keep3[:, 0:LAST_SCATTER])
 
         out_rows = out_0.rearrange("(w t) c -> w t c", t=LANES)
-        cuts = list(zip(PAIR_CUTS, PAIR_CUTS[1:]))
-        pairs = {first: pool.tile([P, 2, stop - first, 2], BF16, name=f"pairs{first}") for first, stop in cuts}
+        pairs = pool.tile([P, TOKENS * LANES], BF16, name="pairs")
 
         def finish(t):
             nc.sync.dma_start(out=out_rows[:, t, :], in_=windows[t][:])
-            for first, stop in cuts:
-                nc.vector.tensor_copy(out=pairs[first][:, t // 2, :, t % 2], in_=windows[t][:, first:stop])
+            cuts = PAIR_CUTS if t == LANES - 1 else (0, TOKENS)
+            for first, stop in zip(cuts, cuts[1:]):
+                nc.vector.tensor_copy(
+                    out=pairs[:].rearrange("p (u c e) -> p u c e", u=2, e=2)[:, t // 2, first:stop, t % 2],
+                    in_=windows[t][:, first:stop],
+                )
 
         for t in (0, 2, 1, 3):
             finish(t)
@@ -178,29 +194,31 @@ def tile_attend_gmerge_pl_kernel(tc, W, dz, wk, wg, koffs, goffs, out_0, out_1, 
         grouped_out = {first: pool.tile([P, (stop - first) * LANES], BF16, name=f"grouped_out{first}", align_bytes=64) for first, stop in stores}
 
         def weave(copy, dtype, first, stop):
-            cut = max(c for c in pairs if c <= first)
             store = max(c for c in grouped_out if c <= first)
-            words = pairs[cut][:].rearrange("p u c e -> p (u c e)").bitcast(dtype).rearrange("p (u c) -> p c u", u=2)
+            words = pairs[:].bitcast(dtype).rearrange("p (u c) -> p c u", u=2)
             copy(
                 out=grouped_out[store][:].bitcast(dtype).rearrange("p (c u) -> p c u", u=2)[:, first - store : stop - store],
-                in_=words[:, first - cut : stop - cut],
+                in_=words[:, first:stop],
             )
+
+        out_codes = {first: pool.tile([P, stop - first], U32, name=f"out_codes{first}", align_bytes=64) for first, stop in stores}
 
         def quantize_tokens(first, stop):
             depth, column = divmod(first, PLANE)
-            codes = pool.tile([P, stop - first], U32, name=f"out_codes{first}", align_bytes=64)
+            store = max(c for c in grouped_out if c <= first)
             nc.vector.quantize_mx(
-                out=codes[:].bitcast(E4M3),
+                out=out_codes[store][:, first - store : stop - store].bitcast(E4M3),
                 scales=out_scales[4 * depth : P, column : column + stop - first],
-                in_=grouped_out[first][:],
+                in_=grouped_out[store][:, (first - store) * LANES : (stop - store) * LANES],
             )
-            nc.sync.dma_start(out=out_words[:, first:stop], in_=codes[:].bitcast(I32))
+            if (store, stop) in stores:
+                nc.sync.dma_start(out=out_words[:, store:stop], in_=out_codes[store][:].bitcast(I32))
 
-        for first, stop in ((0, 256), (256, 512), (512, 1024), (1024, 1536), (1536, 1792)):
+        for first, stop in ((0, 128), (128, 512), (512, 1024), (1024, 1280), (1280, 1536), (1536, 1664), (1664, 1792)):
             weave(nc.scalar.copy, U32, first, stop)
         weave(nc.vector.tensor_copy, I32, 1792, 2048)
-        for s in (0, 1, 4, 2, 3):
-            quantize_tokens(*stores[s])
+        for first, stop in ((0, 512), (1792, 2048), (512, 1024), (1024, 1280), (1280, 1536), (1536, 1664), (1664, 1792)):
+            quantize_tokens(first, stop)
         scale_rows = out_2.rearrange("a b c -> (a b) c").bitcast(I32).rearrange("b (c w) -> c b w", c=2)
         for q in range(4):
             nc.sync.dma_start(

@@ -23,7 +23,7 @@ HALF = 256
 PAIR_CUTS = (0, 128, 512, 1024, 2048)
 PLANE = 1024
 VECTOR_WORDS = 88
-LAST_SCATTER = 384
+LAST_SCATTER = 352
 VECTOR_ZEROES = 768
 
 FLOPS = 2 * 512 * 512 * 512

@@ -20,10 +20,10 @@ MERGED = 512
 FEATURES = 512
 TOKENS = 2048
 HALF = 256
-PAIR_CUTS = (0, 128, 512, 1024, 2048)
 PLANE = 1024
+VECTOR_TOKENS = 320
 VECTOR_WORDS = 88
-LAST_SCATTER = 352
+SCALAR_SHARE = {"gone": 352, "keep": 320}
 VECTOR_ZEROES = 768
 
 FLOPS = 2 * 512 * 512 * 512
@@ -62,7 +62,7 @@ def tile_attend_gmerge_pl_kernel(tc, W, dz, wk, wg, koffs, goffs, out_0, out_1, 
         nc.vector.memset(windows[1][:, 0:1].bitcast(I32), 0)
         nc.gpsimd.memset(windows[1][:, VECTOR_ZEROES:].bitcast(I32), 0)
 
-        zeros = pool.tile([P, MERGED - LAST_SCATTER], F32, name="zeros")
+        zeros = pool.tile([P, MERGED - min(SCALAR_SHARE.values())], F32, name="zeros")
         nc.vector.memset(zeros[:], 0.0)
 
         dz_codes = pool.tile([P, MERGED], U32, name="dz_codes", align_bytes=64)
@@ -143,8 +143,12 @@ def tile_attend_gmerge_pl_kernel(tc, W, dz, wk, wg, koffs, goffs, out_0, out_1, 
             scalar_scatter(windows[t], side, columns, weigh(accs[t][:], side, columns, f"{side[2]}{t}_{columns.start}")[:])
 
         def rest_by_vector(side, weighed):
-            rest = slice(LAST_SCATTER, MERGED)
-            nc.vector.tensor_tensor(places(windows[3], side, rest), weighed[:, rest], zeros[:], ADD)
+            rest = slice(SCALAR_SHARE[side[2]], MERGED)
+            nc.vector.tensor_tensor(places(windows[3], side, rest), weighed[:, rest], zeros[:, 0 : rest.stop - rest.start], ADD)
+
+        def share_by_scalar(side, weighed):
+            share = slice(0, SCALAR_SHARE[side[2]])
+            scalar_scatter(windows[3], side, share, weighed[:, share])
 
         u2 = pool.tile([P, MERGED], F32, name="u2")
         by_scalar(0, keep, early)
@@ -168,56 +172,59 @@ def tile_attend_gmerge_pl_kernel(tc, W, dz, wk, wg, koffs, goffs, out_0, out_1, 
         rest_by_vector(gone, gone3)
         vector_scatter(windows[2], keep, whole, u2[:])
         rest_by_vector(keep, keep3)
-        scalar_scatter(windows[3], gone, slice(0, LAST_SCATTER), gone3[:, 0:LAST_SCATTER])
+        share_by_scalar(gone, gone3)
         by_scalar(1, gone, late)
         vector_scatter(windows[2], gone, late, u2[:, late])
-        scalar_scatter(windows[3], keep, slice(0, LAST_SCATTER), keep3[:, 0:LAST_SCATTER])
+        share_by_scalar(keep, keep3)
 
         out_rows = out_0.rearrange("(w t) c -> w t c", t=LANES)
         pairs = pool.tile([P, TOKENS * LANES], BF16, name="pairs")
 
-        def finish(t):
-            nc.sync.dma_start(out=out_rows[:, t, :], in_=windows[t][:])
-            cuts = PAIR_CUTS if t == LANES - 1 else (0, TOKENS)
-            for first, stop in zip(cuts, cuts[1:]):
-                nc.vector.tensor_copy(
-                    out=pairs[:].rearrange("p (u c e) -> p u c e", u=2, e=2)[:, t // 2, first:stop, t % 2],
-                    in_=windows[t][:, first:stop],
-                )
+        def round_into_pairs(t, first, stop):
+            nc.vector.tensor_copy(
+                out=pairs[:].rearrange("p (u c e) -> p u c e", u=2, e=2)[:, t // 2, first:stop, t % 2],
+                in_=windows[t][:, first:stop],
+            )
 
-        for t in (0, 2, 1, 3):
-            finish(t)
+        for t in (0, 2, 1):
+            nc.sync.dma_start(out=out_rows[:, t, :], in_=windows[t][:])
+            round_into_pairs(t, 0, TOKENS)
+        nc.sync.dma_start(out=out_rows[:, 3, :], in_=windows[3][:])
 
         out_words = out_1.rearrange("a p c t -> (a p) (c t)").bitcast(I32)
         out_scales = pool.tile([P, PLANE], U8, name="out_scales", align_bytes=64)
         stores = ((0, 512), (512, 1024), (1024, 1536), (1536, 1792), (1792, 2048))
-        grouped_out = {first: pool.tile([P, (stop - first) * LANES], BF16, name=f"grouped_out{first}", align_bytes=64) for first, stop in stores}
+        grouped_out = pool.tile([P, TOKENS * LANES], BF16, name="grouped_out", align_bytes=64)
+        out_codes = {first: pool.tile([P, stop - first], U32, name=f"out_codes{first}", align_bytes=64) for first, stop in stores}
 
         def weave(copy, dtype, first, stop):
-            store = max(c for c in grouped_out if c <= first)
-            words = pairs[:].bitcast(dtype).rearrange("p (u c) -> p c u", u=2)
             copy(
-                out=grouped_out[store][:].bitcast(dtype).rearrange("p (c u) -> p c u", u=2)[:, first - store : stop - store],
-                in_=words[:, first:stop],
+                out=grouped_out[:].bitcast(dtype).rearrange("p (c u) -> p c u", u=2)[:, first:stop],
+                in_=pairs[:].bitcast(dtype).rearrange("p (u c) -> p c u", u=2)[:, first:stop],
             )
-
-        out_codes = {first: pool.tile([P, stop - first], U32, name=f"out_codes{first}", align_bytes=64) for first, stop in stores}
 
         def quantize_tokens(first, stop):
             depth, column = divmod(first, PLANE)
-            store = max(c for c in grouped_out if c <= first)
+            store = max(c for c in out_codes if c <= first)
             nc.vector.quantize_mx(
                 out=out_codes[store][:, first - store : stop - store].bitcast(E4M3),
                 scales=out_scales[4 * depth : P, column : column + stop - first],
-                in_=grouped_out[store][:, (first - store) * LANES : (stop - store) * LANES],
+                in_=grouped_out[:, first * LANES : stop * LANES],
             )
             if (store, stop) in stores:
                 nc.sync.dma_start(out=out_words[:, store:stop], in_=out_codes[store][:].bitcast(I32))
 
-        for first, stop in ((0, 128), (128, 512), (512, 1024), (1024, 1280), (1280, 1536), (1536, 1664), (1664, 1792)):
+        second = VECTOR_TOKENS + 128
+        for first, stop in ((VECTOR_TOKENS, second), (second, 768), (0, VECTOR_TOKENS), (768, 1280)):
+            round_into_pairs(3, first, stop)
+        weave(nc.vector.tensor_copy, I32, 0, VECTOR_TOKENS)
+        round_into_pairs(3, 1280, 2048)
+        last_cuts = (1280, 1536, 1792, 1920, 2048)
+        cuts = (VECTOR_TOKENS, second, 768) + last_cuts
+        for first, stop in zip(cuts, cuts[1:]):
             weave(nc.scalar.copy, U32, first, stop)
-        weave(nc.vector.tensor_copy, I32, 1792, 2048)
-        for first, stop in ((0, 512), (1792, 2048), (512, 1024), (1024, 1280), (1280, 1536), (1536, 1664), (1664, 1792)):
+        cuts = (0, 512, 1024) + last_cuts
+        for first, stop in zip(cuts, cuts[1:]):
             quantize_tokens(first, stop)
         scale_rows = out_2.rearrange("a b c -> (a b) c").bitcast(I32).rearrange("b (c w) -> c b w", c=2)
         for q in range(4):

@@ -214,14 +214,13 @@ def tile_attend_gmerge_pl_kernel(tc, W, dz, wk, wg, koffs, goffs, out_0, out_1, 
             if (store, stop) in stores:
                 nc.sync.dma_start(out=out_words[:, store:stop], in_=out_codes[store][:].bitcast(I32))
 
-        second = VECTOR_TOKENS + 128
-        for first, stop in ((VECTOR_TOKENS, second), (second, 768), (0, VECTOR_TOKENS), (768, 1280)):
-            round_into_pairs(3, first, stop)
-        weave(nc.vector.tensor_copy, I32, 0, VECTOR_TOKENS)
-        round_into_pairs(3, 1280, 2048)
+        own = (512, 512 + VECTOR_TOKENS)
+        early_pieces = ((0, 128), (128, 512), (own[1], 1280))
         last_cuts = (1280, 1536, 1792, 1920, 2048)
-        cuts = (VECTOR_TOKENS, second, 768) + last_cuts
-        for first, stop in zip(cuts, cuts[1:]):
+        for first, stop in early_pieces + (own, (1280, 2048)):
+            round_into_pairs(3, first, stop)
+        weave(nc.vector.tensor_copy, I32, *own)
+        for first, stop in early_pieces + tuple(zip(last_cuts, last_cuts[1:])):
             weave(nc.scalar.copy, U32, first, stop)
         cuts = (0, 512, 1024) + last_cuts
         for first, stop in zip(cuts, cuts[1:]):

@@ -21,6 +21,7 @@ FEATURES = 512
 TOKENS = 2048
 HALF = 256
 PLANE = 1024
+SCALAR_QUADS = 20
 VECTOR_TOKENS = 320
 VECTOR_WORDS = 88
 SCALAR_SHARE = {"gone": 352, "keep": 320}
@@ -48,10 +49,11 @@ def tile_attend_gmerge_pl_kernel(tc, W, dz, wk, wg, koffs, goffs, out_0, out_1, 
         nc.sync.dma_start(out=w_raw[0][:], in_=w_rows[:, 0:2, :])
         nc.sync.dma_start(out=w_raw[1][:], in_=w_rows[:, 2:4, :])
         nc.sync.dma_start(keep_list[:], koffs)
-        nc.sync.dma_start(out=keep_weight[:], in_=wk)
+        nc.sync.dma_start(out=keep_weight[:, early], in_=wk[:, early])
         nc.sync.dma_start(out=dz_raw[1][:], in_=dz_rows[:, :, late])
         nc.sync.dma_start(gone_list[:], goffs)
         nc.sync.dma_start(out=gone_weight[:], in_=wg)
+        nc.sync.dma_start(out=keep_weight[:, late], in_=wk[:, late])
         keep, gone = (keep_list, keep_weight, "keep"), (gone_list, gone_weight, "gone")
 
         windows = [pool.tile([P, TOKENS], F32, name=f"window{t}") for t in range(3)]
@@ -71,13 +73,13 @@ def tile_attend_gmerge_pl_kernel(tc, W, dz, wk, wg, koffs, goffs, out_0, out_1, 
         w_scales = pool.tile([P, FEATURES], U8, name="w_scales", align_bytes=64)
         w_grouped = [pool.tile([P, 2, P, LANES], BF16, name=f"w_grouped{u}", align_bytes=64) for u in range(2)]
 
-        def group_dz(copy, h):
-            grouped = pool.tile([P, HALF * LANES], BF16, name=f"dz_grouped{h}", align_bytes=64)
+        dz_grouped = [pool.tile([P, HALF * LANES], BF16, name=f"dz_grouped{h}", align_bytes=64) for h in range(2)]
+
+        def group_dz(copy, h, quads=slice(0, HALF // 4)):
             copy(
-                out=grouped[:].rearrange("p (c i j) -> p c j i", i=4, j=LANES),
-                in_=dz_raw[h][:].rearrange("p j (c i) -> p c j i", i=4),
+                out=dz_grouped[h][:].rearrange("p (c i j) -> p c j i", i=4, j=LANES)[:, quads],
+                in_=dz_raw[h][:].rearrange("p j (c i) -> p c j i", i=4)[:, quads],
             )
-            return grouped
 
         def group_w(copy, u, a, words=slice(0, P)):
             copy(
@@ -128,7 +130,8 @@ def tile_attend_gmerge_pl_kernel(tc, W, dz, wk, wg, koffs, goffs, out_0, out_1, 
         def vector_scatter(window, side, columns, u):
             nc.vector.tensor_tensor(places(window, side, columns), u, side[1][:, columns], MULT)
 
-        quantize_dz(early, group_dz(nc.scalar.copy, 0))
+        group_dz(nc.scalar.copy, 0)
+        quantize_dz(early, dz_grouped[0])
         group_w(nc.vector.tensor_copy, 0, 0)
         group_w(nc.scalar.copy, 1, 0)
         group_w(nc.vector.tensor_copy, 0, 1, slice(0, VECTOR_WORDS))
@@ -151,11 +154,12 @@ def tile_attend_gmerge_pl_kernel(tc, W, dz, wk, wg, koffs, goffs, out_0, out_1, 
             scalar_scatter(windows[3], side, share, weighed[:, share])
 
         u2 = pool.tile([P, MERGED], F32, name="u2")
+        group_dz(nc.scalar.copy, 1, slice(0, SCALAR_QUADS))
         by_scalar(0, keep, early)
         by_scalar(1, keep, early)
-        dz_late = group_dz(nc.vector.tensor_copy, 1)
+        group_dz(nc.vector.tensor_copy, 1, slice(SCALAR_QUADS, HALF // 4))
         nc.vector.tensor_copy(out=u2[:, early], in_=accs[2][:])
-        quantize_dz(late, dz_late)
+        quantize_dz(late, dz_grouped[1])
         windows.append(pool.tile([P, TOKENS], F32, name="dz_grouped1", align_bytes=64))
         nc.gpsimd.memset(windows[3][:].bitcast(I32), 0)
         by_scalar(0, gone, early)

@@ -22,9 +22,11 @@ TOKENS = 2048
 HALF = 256
 PLANE = 1024
 SCALAR_QUADS = 20
-VECTOR_TOKENS = 320
+VECTOR_TOKENS = 352
+FILL_TOKENS = 192
+PAIR_ROW = TOKENS - FILL_TOKENS + HALF
 VECTOR_WORDS = 88
-SCALAR_SHARE = {"gone": 352, "keep": 320}
+SCALAR_SHARE = {"gone": 320, "keep": 320}
 VECTOR_ZEROES = 768
 
 FLOPS = 2 * 512 * 512 * 512
@@ -177,23 +179,27 @@ def tile_attend_gmerge_pl_kernel(tc, W, dz, wk, wg, koffs, goffs, out_0, out_1, 
         vector_scatter(windows[2], keep, whole, u2[:])
         rest_by_vector(keep, keep3)
         share_by_scalar(gone, gone3)
-        by_scalar(1, gone, late)
+        pairs = pool.tile([P, 2 * PAIR_ROW], F32, name="pairs")
+        gone1 = pairs[:, PAIR_ROW - HALF : PAIR_ROW]
+        nc.vector.tensor_tensor(gone1, accs[1][:], gone_weight[:, late], MULT)
+        scalar_scatter(windows[1], gone, late, gone1)
         vector_scatter(windows[2], gone, late, u2[:, late])
         share_by_scalar(keep, keep3)
 
         out_rows = out_0.rearrange("(w t) c -> w t c", t=LANES)
-        pairs = pool.tile([P, TOKENS * LANES], BF16, name="pairs")
 
-        def round_into_pairs(t, first, stop):
-            nc.vector.tensor_copy(
-                out=pairs[:].rearrange("p (u c e) -> p u c e", u=2, e=2)[:, t // 2, first:stop, t % 2],
+        def round_into_pairs(t, first, stop, copy=nc.vector.tensor_copy):
+            copy(
+                out=pairs[:].bitcast(BF16).rearrange("p (u c e) -> p u c e", u=2, e=2)[:, t // 2, first:stop, t % 2],
                 in_=windows[t][:, first:stop],
             )
 
         for t in (0, 2, 1):
             nc.sync.dma_start(out=out_rows[:, t, :], in_=windows[t][:])
-            round_into_pairs(t, 0, TOKENS)
+            round_into_pairs(t, 0, TOKENS if t == 2 else TOKENS - FILL_TOKENS)
         nc.sync.dma_start(out=out_rows[:, 3, :], in_=windows[3][:])
+        for t in (0, 1):
+            round_into_pairs(t, TOKENS - FILL_TOKENS, TOKENS, nc.scalar.copy)
 
         out_words = out_1.rearrange("a p c t -> (a p) (c t)").bitcast(I32)
         out_scales = pool.tile([P, PLANE], U8, name="out_scales", align_bytes=64)

@@ -203,7 +203,7 @@ def tile_attend_gmerge_pl_kernel(tc, W, dz, wk, wg, koffs, goffs, out_0, out_1, 
 
         out_words = out_1.rearrange("a p c t -> (a p) (c t)").bitcast(I32)
         out_scales = pool.tile([P, PLANE], U8, name="out_scales", align_bytes=64)
-        stores = ((0, 512), (512, 1024), (1024, 1536), (1536, 1792), (1792, 2048))
+        stores = ((0, 512), (512, 1024), (1024, 1536), (1536, 2048))
         grouped_out = pool.tile([P, TOKENS * LANES], BF16, name="grouped_out", align_bytes=64)
         out_codes = {first: pool.tile([P, stop - first], U32, name=f"out_codes{first}", align_bytes=64) for first, stop in stores}
 

@@ -22,8 +22,8 @@ TOKENS = 2048
 HALF = 256
 PLANE = 1024
 SCALAR_QUADS = 20
-VECTOR_TOKENS = 352
-FILL_TOKENS = 192
+VECTOR_TOKENS = 384
+FILL_TOKENS = 224
 PAIR_ROW = TOKENS - FILL_TOKENS + HALF
 VECTOR_WORDS = 88
 SCALAR_SHARE = {"gone": 320, "keep": 320}

@@ -11,7 +11,6 @@ U8 = mybir.dt.uint8
 E4M3 = mybir.dt.float8_e4m3fn_x4
 E5M2 = mybir.dt.float8_e5m2_x4
 MULT = mybir.AluOpType.mult
-ADD = mybir.AluOpType.add
 COPY = mybir.ActivationFunctionType.Copy
 
 P = 128
@@ -23,10 +22,9 @@ HALF = 256
 PLANE = 1024
 SCALAR_QUADS = 20
 VECTOR_TOKENS = 384
-FILL_TOKENS = 224
-PAIR_ROW = TOKENS - FILL_TOKENS + HALF
+FILL_TOKENS = 288
+PAIR_ROW = TOKENS - FILL_TOKENS + MERGED
 VECTOR_WORDS = 88
-SCALAR_SHARE = {"gone": 320, "keep": 320}
 VECTOR_ZEROES = 768
 
 FLOPS = 2 * 512 * 512 * 512
@@ -66,8 +64,8 @@ def tile_attend_gmerge_pl_kernel(tc, W, dz, wk, wg, koffs, goffs, out_0, out_1, 
         nc.vector.memset(windows[1][:, 0:1].bitcast(I32), 0)
         nc.gpsimd.memset(windows[1][:, VECTOR_ZEROES:].bitcast(I32), 0)
 
-        zeros = pool.tile([P, MERGED - min(SCALAR_SHARE.values())], F32, name="zeros")
-        nc.vector.memset(zeros[:], 0.0)
+        ones = pool.tile([P, 1], F32, name="ones")
+        nc.vector.memset(ones[:], 1.0)
 
         dz_codes = pool.tile([P, MERGED], U32, name="dz_codes", align_bytes=64)
         dz_scales = pool.tile([P, MERGED], U8, name="dz_scales", align_bytes=64)
@@ -118,11 +116,6 @@ def tile_attend_gmerge_pl_kernel(tc, W, dz, wk, wg, koffs, goffs, out_0, out_1, 
             nc.vector.tensor_tensor(weighed[:], acc, side[1][:, columns], MULT)
             return weighed
 
-        def to_sbuf(acc, name):
-            u = pool.tile([P, acc.shape[1]], F32, name=name)
-            nc.vector.tensor_copy(out=u[:], in_=acc)
-            return u
-
         def places(window, side, columns):
             return window[:].indirect(side[0][:, columns.start // 16 : columns.stop // 16])
 
@@ -147,14 +140,6 @@ def tile_attend_gmerge_pl_kernel(tc, W, dz, wk, wg, koffs, goffs, out_0, out_1, 
         def by_scalar(t, side, columns):
             scalar_scatter(windows[t], side, columns, weigh(accs[t][:], side, columns, f"{side[2]}{t}_{columns.start}")[:])
 
-        def rest_by_vector(side, weighed):
-            rest = slice(SCALAR_SHARE[side[2]], MERGED)
-            nc.vector.tensor_tensor(places(windows[3], side, rest), weighed[:, rest], zeros[:, 0 : rest.stop - rest.start], ADD)
-
-        def share_by_scalar(side, weighed):
-            share = slice(0, SCALAR_SHARE[side[2]])
-            scalar_scatter(windows[3], side, share, weighed[:, share])
-
         u2 = pool.tile([P, MERGED], F32, name="u2")
         group_dz(nc.scalar.copy, 1, slice(0, SCALAR_QUADS))
         by_scalar(0, keep, early)
@@ -167,24 +152,23 @@ def tile_attend_gmerge_pl_kernel(tc, W, dz, wk, wg, koffs, goffs, out_0, out_1, 
         by_scalar(0, gone, early)
         by_scalar(1, gone, early)
         vector_scatter(windows[2], gone, early, u2[:, early])
-        accs = [product(t, late, f"acc{t}_late") for t in range(3)]
+        accs[2] = product(2, late, "acc2_late")
+        accs[0] = product(0, late, "acc0_late")
         acc3 = product(3, whole, "acc3")
-        by_scalar(0, keep, late)
-        by_scalar(1, keep, late)
-        nc.vector.tensor_copy(out=u2[:, late], in_=accs[2][:])
-        gone3 = weigh(acc3[:], gone, whole, "gone3")
-        keep3 = weigh(acc3[:], keep, whole, "keep3")
-        by_scalar(0, gone, late)
-        rest_by_vector(gone, gone3)
-        vector_scatter(windows[2], keep, whole, u2[:])
-        rest_by_vector(keep, keep3)
-        share_by_scalar(gone, gone3)
+        accs[1] = product(1, late, "acc1_late")
         pairs = pool.tile([P, 2 * PAIR_ROW], F32, name="pairs")
-        gone1 = pairs[:, PAIR_ROW - HALF : PAIR_ROW]
-        nc.vector.tensor_tensor(gone1, accs[1][:], gone_weight[:, late], MULT)
-        scalar_scatter(windows[1], gone, late, gone1)
+        u3 = pairs[:, PAIR_ROW - MERGED : PAIR_ROW]
+        nc.vector.tensor_copy(out=u2[:, late], in_=accs[2][:])
+        by_scalar(0, keep, late)
+        nc.scalar.copy(out=u3, in_=acc3[:])
+        vector_scatter(windows[2], keep, whole, u2[:])
+        by_scalar(1, keep, late)
         vector_scatter(windows[2], gone, late, u2[:, late])
-        share_by_scalar(keep, keep3)
+        by_scalar(0, gone, late)
+        by_scalar(1, gone, late)
+        keep3 = weigh(acc3[:], keep, whole, "keep3")
+        vector_scatter(windows[3], gone, whole, u3)
+        nc.scalar.activation(places(windows[3], keep, whole), keep3[:], COPY, scale=ones[:])
 
         out_rows = out_0.rearrange("(w t) c -> w t c", t=LANES)
 
@@ -194,7 +178,7 @@ def tile_attend_gmerge_pl_kernel(tc, W, dz, wk, wg, koffs, goffs, out_0, out_1, 
                 in_=windows[t][:, first:stop],
             )
 
-        for t in (0, 2, 1):
+        for t in (2, 0, 1):
             nc.sync.dma_start(out=out_rows[:, t, :], in_=windows[t][:])
             round_into_pairs(t, 0, TOKENS if t == 2 else TOKENS - FILL_TOKENS)
         nc.sync.dma_start(out=out_rows[:, 3, :], in_=windows[3][:])
@@ -203,7 +187,7 @@ def tile_attend_gmerge_pl_kernel(tc, W, dz, wk, wg, koffs, goffs, out_0, out_1, 
 
         out_words = out_1.rearrange("a p c t -> (a p) (c t)").bitcast(I32)
         out_scales = pool.tile([P, PLANE], U8, name="out_scales", align_bytes=64)
-        stores = ((0, 512), (512, 1024), (1024, 1536), (1536, 2048))
+        stores = ((0, 512), (512, 1024), (1024, 1536), (1536, 1792), (1792, 2048))
         grouped_out = pool.tile([P, TOKENS * LANES], BF16, name="grouped_out", align_bytes=64)
         out_codes = {first: pool.tile([P, stop - first], U32, name=f"out_codes{first}", align_bytes=64) for first, stop in stores}
 

@@ -11,6 +11,7 @@ U8 = mybir.dt.uint8
 E4M3 = mybir.dt.float8_e4m3fn_x4
 E5M2 = mybir.dt.float8_e5m2_x4
 MULT = mybir.AluOpType.mult
+ADD = mybir.AluOpType.add
 COPY = mybir.ActivationFunctionType.Copy
 
 P = 128
@@ -22,7 +23,8 @@ HALF = 256
 PLANE = 1024
 SCALAR_QUADS = 20
 VECTOR_TOKENS = 384
-FILL_TOKENS = 288
+FILL_TOKENS = 160
+POOL_TOKENS = 512
 PAIR_ROW = TOKENS - FILL_TOKENS + MERGED
 VECTOR_WORDS = 88
 VECTOR_ZEROES = 768
@@ -64,8 +66,8 @@ def tile_attend_gmerge_pl_kernel(tc, W, dz, wk, wg, koffs, goffs, out_0, out_1, 
         nc.vector.memset(windows[1][:, 0:1].bitcast(I32), 0)
         nc.gpsimd.memset(windows[1][:, VECTOR_ZEROES:].bitcast(I32), 0)
 
-        ones = pool.tile([P, 1], F32, name="ones")
-        nc.vector.memset(ones[:], 1.0)
+        unit = pool.tile([P, 1], F32, name="unit")
+        nc.vector.memset(unit[:], -0.0)
 
         dz_codes = pool.tile([P, MERGED], U32, name="dz_codes", align_bytes=64)
         dz_scales = pool.tile([P, MERGED], U8, name="dz_scales", align_bytes=64)
@@ -157,30 +159,34 @@ def tile_attend_gmerge_pl_kernel(tc, W, dz, wk, wg, koffs, goffs, out_0, out_1, 
         acc3 = product(3, whole, "acc3")
         accs[1] = product(1, late, "acc1_late")
         pairs = pool.tile([P, 2 * PAIR_ROW], F32, name="pairs")
-        u3 = pairs[:, PAIR_ROW - MERGED : PAIR_ROW]
+        u3 = pool.tile([P, MERGED], F32, name="u3")
+        keep3 = pairs[:, PAIR_ROW - MERGED : PAIR_ROW]
+
+        def lane(t, first, stop):
+            return pairs[:].bitcast(BF16).rearrange("p (u c e) -> p u c e", u=2, e=2)[:, t // 2, first:stop, t % 2]
+
         nc.vector.tensor_copy(out=u2[:, late], in_=accs[2][:])
         by_scalar(0, keep, late)
-        nc.scalar.copy(out=u3, in_=acc3[:])
+        nc.scalar.copy(out=u3[:], in_=acc3[:])
         vector_scatter(windows[2], keep, whole, u2[:])
         by_scalar(1, keep, late)
         vector_scatter(windows[2], gone, late, u2[:, late])
+        nc.gpsimd.tensor_scalar(lane(2, TOKENS - POOL_TOKENS, TOKENS), windows[2][:, TOKENS - POOL_TOKENS :], 1.0, unit[:], MULT, ADD)
+        nc.gpsimd.memset(unit[:], 1.0)
         by_scalar(0, gone, late)
         by_scalar(1, gone, late)
-        keep3 = weigh(acc3[:], keep, whole, "keep3")
-        vector_scatter(windows[3], gone, whole, u3)
-        nc.scalar.activation(places(windows[3], keep, whole), keep3[:], COPY, scale=ones[:])
+        nc.vector.tensor_tensor(keep3, acc3[:], keep_weight[:], MULT)
+        vector_scatter(windows[3], gone, whole, u3[:])
+        nc.scalar.activation(places(windows[3], keep, whole), keep3, COPY, scale=unit[:])
 
         out_rows = out_0.rearrange("(w t) c -> w t c", t=LANES)
 
         def round_into_pairs(t, first, stop, copy=nc.vector.tensor_copy):
-            copy(
-                out=pairs[:].bitcast(BF16).rearrange("p (u c e) -> p u c e", u=2, e=2)[:, t // 2, first:stop, t % 2],
-                in_=windows[t][:, first:stop],
-            )
+            copy(out=lane(t, first, stop), in_=windows[t][:, first:stop])
 
         for t in (2, 0, 1):
             nc.sync.dma_start(out=out_rows[:, t, :], in_=windows[t][:])
-            round_into_pairs(t, 0, TOKENS if t == 2 else TOKENS - FILL_TOKENS)
+            round_into_pairs(t, 0, TOKENS - (POOL_TOKENS if t == 2 else FILL_TOKENS))
         nc.sync.dma_start(out=out_rows[:, 3, :], in_=windows[3][:])
         for t in (0, 1):
             round_into_pairs(t, TOKENS - FILL_TOKENS, TOKENS, nc.scalar.copy)

@@ -142,17 +142,24 @@ def tile_attend_gmerge_pl_kernel(tc, W, dz, wk, wg, koffs, goffs, out_0, out_1, 
         def by_scalar(t, side, columns):
             scalar_scatter(windows[t], side, columns, weigh(accs[t][:], side, columns, f"{side[2]}{t}_{columns.start}")[:])
 
-        u2 = pool.tile([P, MERGED], F32, name="u2")
+        u2 = dz_raw[1][:].rearrange("p j i -> p (j i)")[:, 0:MERGED]
+
+        def pool_round(out, in_):
+            nc.gpsimd.tensor_scalar(out, in_, 1.0, -0.0, MULT, ADD)
+
         group_dz(nc.scalar.copy, 1, slice(0, SCALAR_QUADS))
+        pool_round(
+            dz_grouped[1][:].rearrange("p (i j) -> p i j", j=LANES)[:, 4 * SCALAR_QUADS :],
+            dz_raw[1][:].rearrange("p j i -> p i j")[:, 4 * SCALAR_QUADS :],
+        )
         by_scalar(0, keep, early)
         by_scalar(1, keep, early)
-        group_dz(nc.vector.tensor_copy, 1, slice(SCALAR_QUADS, HALF // 4))
+        by_scalar(0, gone, early)
+        by_scalar(1, gone, early)
         nc.vector.tensor_copy(out=u2[:, early], in_=accs[2][:])
         quantize_dz(late, dz_grouped[1])
         windows.append(pool.tile([P, TOKENS], F32, name="dz_grouped1", align_bytes=64))
         nc.gpsimd.memset(windows[3][:].bitcast(I32), 0)
-        by_scalar(0, gone, early)
-        by_scalar(1, gone, early)
         vector_scatter(windows[2], gone, early, u2[:, early])
         accs[2] = product(2, late, "acc2_late")
         accs[0] = product(0, late, "acc0_late")
@@ -168,7 +175,7 @@ def tile_attend_gmerge_pl_kernel(tc, W, dz, wk, wg, koffs, goffs, out_0, out_1, 
         nc.vector.tensor_copy(out=u2[:, late], in_=accs[2][:])
         by_scalar(0, keep, late)
         nc.scalar.copy(out=u3[:], in_=acc3[:])
-        vector_scatter(windows[2], keep, whole, u2[:])
+        vector_scatter(windows[2], keep, whole, u2)
         by_scalar(1, keep, late)
         vector_scatter(windows[2], gone, late, u2[:, late])
         nc.gpsimd.tensor_scalar(lane(2, TOKENS - POOL_TOKENS, TOKENS), windows[2][:, TOKENS - POOL_TOKENS :], 1.0, unit[:], MULT, ADD)

@@ -24,7 +24,7 @@ PLANE = 1024
 SCALAR_QUADS = 20
 VECTOR_TOKENS = 384
 FILL_TOKENS = 160
-POOL_TOKENS = 512
+POOL_TOKENS = 704
 PAIR_ROW = TOKENS - FILL_TOKENS + MERGED
 VECTOR_WORDS = 88
 VECTOR_ZEROES = 768
@@ -174,7 +174,7 @@ def tile_attend_gmerge_pl_kernel(tc, W, dz, wk, wg, koffs, goffs, out_0, out_1, 
 
         nc.vector.tensor_copy(out=u2[:, late], in_=accs[2][:])
         by_scalar(0, keep, late)
-        nc.scalar.copy(out=u3[:], in_=acc3[:])
+        nc.scalar.copy(out=u3[:, early], in_=acc3[:, early])
         vector_scatter(windows[2], keep, whole, u2)
         by_scalar(1, keep, late)
         vector_scatter(windows[2], gone, late, u2[:, late])
@@ -182,6 +182,7 @@ def tile_attend_gmerge_pl_kernel(tc, W, dz, wk, wg, koffs, goffs, out_0, out_1, 
         nc.gpsimd.memset(unit[:], 1.0)
         by_scalar(0, gone, late)
         by_scalar(1, gone, late)
+        nc.vector.tensor_copy(out=u3[:, late], in_=acc3[:, late])
         nc.vector.tensor_tensor(keep3, acc3[:], keep_weight[:], MULT)
         vector_scatter(windows[3], gone, whole, u3[:])
         nc.scalar.activation(places(windows[3], keep, whole), keep3, COPY, scale=unit[:])

@@ -23,8 +23,8 @@ HALF = 256
 PLANE = 1024
 SCALAR_QUADS = 20
 VECTOR_TOKENS = 384
-FILL_TOKENS = 160
-POOL_TOKENS = 704
+FILL_TOKENS = 240
+POOL_TOKENS = 640
 PAIR_ROW = TOKENS - FILL_TOKENS + MERGED
 VECTOR_WORDS = 88
 VECTOR_ZEROES = 768
@@ -166,8 +166,8 @@ def tile_attend_gmerge_pl_kernel(tc, W, dz, wk, wg, koffs, goffs, out_0, out_1, 
         acc3 = product(3, whole, "acc3")
         accs[1] = product(1, late, "acc1_late")
         pairs = pool.tile([P, 2 * PAIR_ROW], F32, name="pairs")
-        u3 = pool.tile([P, MERGED], F32, name="u3")
-        keep3 = pairs[:, PAIR_ROW - MERGED : PAIR_ROW]
+        u3 = pairs[:, PAIR_ROW - MERGED : PAIR_ROW]
+        keep3 = pool.tile([P, MERGED], F32, name="keep3")
 
         def lane(t, first, stop):
             return pairs[:].bitcast(BF16).rearrange("p (u c e) -> p u c e", u=2, e=2)[:, t // 2, first:stop, t % 2]
@@ -179,13 +179,13 @@ def tile_attend_gmerge_pl_kernel(tc, W, dz, wk, wg, koffs, goffs, out_0, out_1, 
         by_scalar(1, keep, late)
         vector_scatter(windows[2], gone, late, u2[:, late])
         nc.gpsimd.tensor_scalar(lane(2, TOKENS - POOL_TOKENS, TOKENS), windows[2][:, TOKENS - POOL_TOKENS :], 1.0, unit[:], MULT, ADD)
-        nc.gpsimd.memset(unit[:], 1.0)
         by_scalar(0, gone, late)
         by_scalar(1, gone, late)
-        nc.vector.tensor_copy(out=u3[:, late], in_=acc3[:, late])
-        nc.vector.tensor_tensor(keep3, acc3[:], keep_weight[:], MULT)
-        vector_scatter(windows[3], gone, whole, u3[:])
-        nc.scalar.activation(places(windows[3], keep, whole), keep3, COPY, scale=unit[:])
+        nc.vector.tensor_tensor(u3[:, late], acc3[:, late], unit[:].to_broadcast([P, HALF]), ADD)
+        nc.gpsimd.memset(unit[:], 1.0)
+        nc.vector.tensor_tensor(keep3[:], acc3[:], keep_weight[:], MULT)
+        vector_scatter(windows[3], gone, whole, u3)
+        nc.scalar.activation(places(windows[3], keep, whole), keep3[:], COPY, scale=unit[:])
 
         out_rows = out_0.rearrange("(w t) c -> w t c", t=LANES)
 
@@ -197,7 +197,7 @@ def tile_attend_gmerge_pl_kernel(tc, W, dz, wk, wg, koffs, goffs, out_0, out_1, 
             round_into_pairs(t, 0, TOKENS - (POOL_TOKENS if t == 2 else FILL_TOKENS))
         nc.sync.dma_start(out=out_rows[:, 3, :], in_=windows[3][:])
         for t in (0, 1):
-            round_into_pairs(t, TOKENS - FILL_TOKENS, TOKENS, nc.scalar.copy)
+            nc.scalar.activation(lane(t, TOKENS - FILL_TOKENS, TOKENS), windows[t][:, TOKENS - FILL_TOKENS :], COPY, scale=unit[:])
 
         out_words = out_1.rearrange("a p c t -> (a p) (c t)").bitcast(I32)
         out_scales = pool.tile([P, PLANE], U8, name="out_scales", align_bytes=64)

@@ -50,9 +50,9 @@ def tile_attend_gmerge_pl_kernel(tc, W, dz, wk, wg, koffs, goffs, out_0, out_1, 
         nc.sync.dma_start(out=dz_raw[0][:], in_=dz_rows[:, :, early])
         nc.sync.dma_start(out=w_raw[0][:], in_=w_rows[:, 0:2, :])
         nc.sync.dma_start(out=w_raw[1][:], in_=w_rows[:, 2:4, :])
-        nc.sync.dma_start(keep_list[:], koffs)
         nc.sync.dma_start(out=keep_weight[:, early], in_=wk[:, early])
         nc.sync.dma_start(out=dz_raw[1][:], in_=dz_rows[:, :, late])
+        nc.sync.dma_start(keep_list[:], koffs)
         nc.sync.dma_start(gone_list[:], goffs)
         nc.sync.dma_start(out=gone_weight[:], in_=wg)
         nc.sync.dma_start(out=keep_weight[:, late], in_=wk[:, late])
@@ -178,7 +178,7 @@ def tile_attend_gmerge_pl_kernel(tc, W, dz, wk, wg, koffs, goffs, out_0, out_1, 
         vector_scatter(windows[2], keep, whole, u2)
         by_scalar(1, keep, late)
         vector_scatter(windows[2], gone, late, u2[:, late])
-        nc.gpsimd.tensor_scalar(lane(2, TOKENS - POOL_TOKENS, TOKENS), windows[2][:, TOKENS - POOL_TOKENS :], 1.0, unit[:], MULT, ADD)
+        pool_round(lane(2, TOKENS - POOL_TOKENS, TOKENS), windows[2][:, TOKENS - POOL_TOKENS :])
         by_scalar(0, gone, late)
         by_scalar(1, gone, late)
         nc.vector.tensor_tensor(u3[:, late], acc3[:, late], unit[:].to_broadcast([P, HALF]), ADD)

@@ -21,7 +21,7 @@ FEATURES = 512
 TOKENS = 2048
 HALF = 256
 PLANE = 1024
-SCALAR_QUADS = 20
+SCALAR_QUADS = 26
 VECTOR_TOKENS = 384
 FILL_TOKENS = 240
 POOL_TOKENS = 640

from contextlib import ExitStack

import concourse.mybir as mybir

F32 = mybir.dt.float32
BF16 = mybir.dt.bfloat16
I32 = mybir.dt.int32
U32 = mybir.dt.uint32
U16 = mybir.dt.uint16
U8 = mybir.dt.uint8
E4M3 = mybir.dt.float8_e4m3fn_x4
E5M2 = mybir.dt.float8_e5m2_x4
MULT = mybir.AluOpType.mult
ADD = mybir.AluOpType.add
COPY = mybir.ActivationFunctionType.Copy

P = 128
LANES = 4
MERGED = 512
FEATURES = 512
TOKENS = 2048
HALF = 256
PLANE = 1024
SCALAR_QUADS = 26
VECTOR_TOKENS = 384
FILL_TOKENS = 240
POOL_TOKENS = 640
PAIR_ROW = TOKENS - FILL_TOKENS + MERGED
VECTOR_WORDS = 88
VECTOR_ZEROES = 768

FLOPS = 2 * 512 * 512 * 512


def tile_attend_gmerge_pl_kernel(tc, W, dz, wk, wg, koffs, goffs, out_0, out_1, out_2):
    nc = tc.nc
    with ExitStack() as ctx:
        pool = ctx.enter_context(tc.tile_pool(name="held", bufs=1))
        psum = ctx.enter_context(tc.psum_pool(name="psum", bufs=1))

        early, late, whole = slice(0, HALF), slice(HALF, MERGED), slice(0, MERGED)
        keep_list = pool.tile([P, MERGED // 16], U16, name="keep_list")
        gone_list = pool.tile([P, MERGED // 16], U16, name="gone_list")
        keep_weight = pool.tile([P, MERGED], F32, name="keep_weight")
        gone_weight = pool.tile([P, MERGED], F32, name="gone_weight")
        dz_rows = dz.rearrange("(p j) i -> p j i", j=LANES)
        w_rows = W.rearrange("(p j) d -> p j d", j=LANES)
        dz_raw = [pool.tile([P, LANES, HALF], F32, name=f"dz_raw{h}") for h in range(2)]
        w_raw = [pool.tile([P, 2, FEATURES], F32, name=f"w_raw{a}") for a in range(2)]
        nc.sync.dma_start(out=dz_raw[0][:], in_=dz_rows[:, :, early])
        nc.sync.dma_start(out=w_raw[0][:], in_=w_rows[:, 0:2, :])
        nc.sync.dma_start(out=w_raw[1][:], in_=w_rows[:, 2:4, :])
        nc.sync.dma_start(out=keep_weight[:, early], in_=wk[:, early])
        nc.sync.dma_start(out=dz_raw[1][:], in_=dz_rows[:, :, late])
        nc.sync.dma_start(keep_list[:], koffs)
        nc.sync.dma_start(gone_list[:], goffs)
        nc.sync.dma_start(out=gone_weight[:], in_=wg)
        nc.sync.dma_start(out=keep_weight[:, late], in_=wk[:, late])
        keep, gone = (keep_list, keep_weight, "keep"), (gone_list, gone_weight, "gone")

        windows = [pool.tile([P, TOKENS], F32, name=f"window{t}") for t in range(3)]
        nc.gpsimd.memset(windows[0][:].bitcast(I32), 0)
        nc.vector.memset(windows[2][:, 0 : PLANE - 1].bitcast(I32), 0)
        nc.vector.memset(windows[2][:, PLANE - 1 :].bitcast(I32), 0)
        nc.vector.memset(windows[1][:, 1:VECTOR_ZEROES].bitcast(I32), 0)
        nc.vector.memset(windows[1][:, 0:1].bitcast(I32), 0)
        nc.gpsimd.memset(windows[1][:, VECTOR_ZEROES:].bitcast(I32), 0)

        unit = pool.tile([P, 1], F32, name="unit")
        nc.vector.memset(unit[:], -0.0)

        dz_codes = pool.tile([P, MERGED], U32, name="dz_codes", align_bytes=64)
        dz_scales = pool.tile([P, MERGED], U8, name="dz_scales", align_bytes=64)
        w_codes = pool.tile([P, FEATURES], U32, name="w_codes", align_bytes=64)
        w_scales = pool.tile([P, FEATURES], U8, name="w_scales", align_bytes=64)
        w_grouped = [pool.tile([P, 2, P, LANES], BF16, name=f"w_grouped{u}", align_bytes=64) for u in range(2)]

        dz_grouped = [pool.tile([P, HALF * LANES], BF16, name=f"dz_grouped{h}", align_bytes=64) for h in range(2)]

        def group_dz(copy, h, quads=slice(0, HALF // 4)):
            copy(
                out=dz_grouped[h][:].rearrange("p (c i j) -> p c j i", i=4, j=LANES)[:, quads],
                in_=dz_raw[h][:].rearrange("p j (c i) -> p c j i", i=4)[:, quads],
            )

        def group_w(copy, u, a, words=slice(0, P)):
            copy(
                out=w_grouped[u][:, :, words, 2 * a : 2 * a + 2].rearrange("p e w j -> p w j e"),
                in_=w_raw[a][:].rearrange("p j (w t) -> p w j t", t=LANES)[:, words, :, 2 * u : 2 * u + 2],
            )

        def quantize_dz(columns, grouped):
            nc.vector.quantize_mx(out=dz_codes[:, columns].bitcast(E5M2), scales=dz_scales[:, columns], in_=grouped[:])

        def quantize_w(first, stop):
            u, columns = first // 2, slice(first * P, stop * P)
            nc.vector.quantize_mx(
                out=w_codes[:, columns].bitcast(E4M3),
                scales=w_scales[:, columns],
                in_=w_grouped[u][:, first - 2 * u : stop - 2 * u].rearrange("p e w j -> p (e w j)"),
            )

        def product(t, columns, bank):
            acc = psum.tile([P, columns.stop - columns.start], F32, name=bank)
            nc.tensor.matmul_mx(
                out=acc[:],
                lhsT=w_codes[:, t * P : (t + 1) * P].bitcast(E4M3),
                lhsT_scale=w_scales[:, t * P : (t + 1) * P],
                rhs=dz_codes[:, columns].bitcast(E5M2),
                rhs_scale=dz_scales[:, columns],
                start=True,
                stop=True,
            )
            return acc

        def weigh(acc, side, columns, name):
            weighed = pool.tile([P, columns.stop - columns.start], F32, name=name)
            nc.vector.tensor_tensor(weighed[:], acc, side[1][:, columns], MULT)
            return weighed

        def places(window, side, columns):
            return window[:].indirect(side[0][:, columns.start // 16 : columns.stop // 16])

        def scalar_scatter(window, side, columns, weighed):
            nc.scalar.activation(places(window, side, columns), weighed, COPY)

        def vector_scatter(window, side, columns, u):
            nc.vector.tensor_tensor(places(window, side, columns), u, side[1][:, columns], MULT)

        group_dz(nc.scalar.copy, 0)
        quantize_dz(early, dz_grouped[0])
        group_w(nc.vector.tensor_copy, 0, 0)
        group_w(nc.scalar.copy, 1, 0)
        group_w(nc.vector.tensor_copy, 0, 1, slice(0, VECTOR_WORDS))
        group_w(nc.scalar.copy, 0, 1, slice(VECTOR_WORDS, P))
        group_w(nc.scalar.copy, 1, 1)
        quantize_w(0, 1)
        quantize_w(1, 2)
        quantize_w(2, 4)
        accs = [product(t, early, f"acc{t}_early") for t in range(3)]

        def by_scalar(t, side, columns):
            scalar_scatter(windows[t], side, columns, weigh(accs[t][:], side, columns, f"{side[2]}{t}_{columns.start}")[:])

        u2 = dz_raw[1][:].rearrange("p j i -> p (j i)")[:, 0:MERGED]

        def pool_round(out, in_):
            nc.gpsimd.tensor_scalar(out, in_, 1.0, -0.0, MULT, ADD)

        group_dz(nc.scalar.copy, 1, slice(0, SCALAR_QUADS))
        pool_round(
            dz_grouped[1][:].rearrange("p (i j) -> p i j", j=LANES)[:, 4 * SCALAR_QUADS :],
            dz_raw[1][:].rearrange("p j i -> p i j")[:, 4 * SCALAR_QUADS :],
        )
        by_scalar(0, keep, early)
        by_scalar(1, keep, early)
        by_scalar(0, gone, early)
        by_scalar(1, gone, early)
        nc.vector.tensor_copy(out=u2[:, early], in_=accs[2][:])
        quantize_dz(late, dz_grouped[1])
        windows.append(pool.tile([P, TOKENS], F32, name="dz_grouped1", align_bytes=64))
        nc.gpsimd.memset(windows[3][:].bitcast(I32), 0)
        vector_scatter(windows[2], gone, early, u2[:, early])
        accs[2] = product(2, late, "acc2_late")
        accs[0] = product(0, late, "acc0_late")
        acc3 = product(3, whole, "acc3")
        accs[1] = product(1, late, "acc1_late")
        pairs = pool.tile([P, 2 * PAIR_ROW], F32, name="pairs")
        u3 = pairs[:, PAIR_ROW - MERGED : PAIR_ROW]
        keep3 = pool.tile([P, MERGED], F32, name="keep3")

        def lane(t, first, stop):
            return pairs[:].bitcast(BF16).rearrange("p (u c e) -> p u c e", u=2, e=2)[:, t // 2, first:stop, t % 2]

        nc.vector.tensor_copy(out=u2[:, late], in_=accs[2][:])
        by_scalar(0, keep, late)
        nc.scalar.copy(out=u3[:, early], in_=acc3[:, early])
        vector_scatter(windows[2], keep, whole, u2)
        by_scalar(1, keep, late)
        vector_scatter(windows[2], gone, late, u2[:, late])
        pool_round(lane(2, TOKENS - POOL_TOKENS, TOKENS), windows[2][:, TOKENS - POOL_TOKENS :])
        by_scalar(0, gone, late)
        by_scalar(1, gone, late)
        nc.vector.tensor_tensor(u3[:, late], acc3[:, late], unit[:].to_broadcast([P, HALF]), ADD)
        nc.gpsimd.memset(unit[:], 1.0)
        nc.vector.tensor_tensor(keep3[:], acc3[:], keep_weight[:], MULT)
        vector_scatter(windows[3], gone, whole, u3)
        nc.scalar.activation(places(windows[3], keep, whole), keep3[:], COPY, scale=unit[:])

        out_rows = out_0.rearrange("(w t) c -> w t c", t=LANES)

        def round_into_pairs(t, first, stop, copy=nc.vector.tensor_copy):
            copy(out=lane(t, first, stop), in_=windows[t][:, first:stop])

        for t in (2, 0, 1):
            nc.sync.dma_start(out=out_rows[:, t, :], in_=windows[t][:])
            round_into_pairs(t, 0, TOKENS - (POOL_TOKENS if t == 2 else FILL_TOKENS))
        nc.sync.dma_start(out=out_rows[:, 3, :], in_=windows[3][:])
        for t in (0, 1):
            nc.scalar.activation(lane(t, TOKENS - FILL_TOKENS, TOKENS), windows[t][:, TOKENS - FILL_TOKENS :], COPY, scale=unit[:])

        out_words = out_1.rearrange("a p c t -> (a p) (c t)").bitcast(I32)
        out_scales = pool.tile([P, PLANE], U8, name="out_scales", align_bytes=64)
        stores = ((0, 512), (512, 1024), (1024, 1536), (1536, 1792), (1792, 2048))
        grouped_out = pool.tile([P, TOKENS * LANES], BF16, name="grouped_out", align_bytes=64)
        out_codes = {first: pool.tile([P, stop - first], U32, name=f"out_codes{first}", align_bytes=64) for first, stop in stores}

        def weave(copy, dtype, first, stop):
            copy(
                out=grouped_out[:].bitcast(dtype).rearrange("p (c u) -> p c u", u=2)[:, first:stop],
                in_=pairs[:].bitcast(dtype).rearrange("p (u c) -> p c u", u=2)[:, first:stop],
            )

        def quantize_tokens(first, stop):
            depth, column = divmod(first, PLANE)
            store = max(c for c in out_codes if c <= first)
            nc.vector.quantize_mx(
                out=out_codes[store][:, first - store : stop - store].bitcast(E4M3),
                scales=out_scales[4 * depth : P, column : column + stop - first],
                in_=grouped_out[:, first * LANES : stop * LANES],
            )
            if (store, stop) in stores:
                nc.sync.dma_start(out=out_words[:, store:stop], in_=out_codes[store][:].bitcast(I32))

        own = (512, 512 + VECTOR_TOKENS)
        early_pieces = ((0, 128), (128, 512), (own[1], 1280))
        last_cuts = (1280, 1536, 1792, 1920, 2048)
        for first, stop in early_pieces + (own, (1280, 2048)):
            round_into_pairs(3, first, stop)
        weave(nc.vector.tensor_copy, I32, *own)
        for first, stop in early_pieces + tuple(zip(last_cuts, last_cuts[1:])):
            weave(nc.scalar.copy, U32, first, stop)
        cuts = (0, 512, 1024) + last_cuts
        for first, stop in zip(cuts, cuts[1:]):
            quantize_tokens(first, stop)
        scale_rows = out_2.rearrange("a b c -> (a b) c").bitcast(I32).rearrange("b (c w) -> c b w", c=2)
        for q in range(4):
            nc.sync.dma_start(
                out=scale_rows[:, 4 * q : 4 * q + 4, :],
                in_=out_scales[32 * q : 32 * q + 8, :].bitcast(I32),
            )
